import numpy as np
import ml_dtypes


def mxq(x, axis, fmt="e4m3"):
    dtype, down = {"e4m3": (ml_dtypes.float8_e4m3fn, 7), "e5m2": (ml_dtypes.float8_e5m2, 14)}[fmt]
    v = np.moveaxis(np.asarray(x, np.float32).astype(ml_dtypes.bfloat16).astype(np.float64), axis, -1)
    blocks = v.reshape(v.shape[:-1] + (-1, 32))
    amax = np.abs(blocks).max(-1, keepdims=True)
    byte = np.maximum(np.where(amax > 0, np.frexp(amax)[1] - 1 + 127, 0) - down, 1)
    scale = np.exp2(byte - 127.0)
    codes = (blocks / scale).astype(np.float32).astype(dtype).astype(np.float64)
    return np.moveaxis((codes * scale).reshape(v.shape), -1, axis)


WIDE = False


def mx_kscale(k):
    if not WIDE:
        return np.ones(k)
    levels = np.array([10, -10, 5, -5, 0])
    if k % 512:
        return np.exp2(np.random.permutation(np.resize(levels, k // 32))).repeat(32)
    a = np.empty((k // 512, 16))
    for p in range(k // 512):
        a[p, :8] = np.random.permutation(np.resize(levels, 8))
        for g in range(8):
            far = levels[np.abs(levels - a[p, g]) >= 10]
            a[p, g + 8] = far[np.random.randint(len(far))]
    return np.exp2(a.ravel()).repeat(32)


def f64(x):
    return np.asarray(x).astype(np.float64)


def striped(idx):
    return np.tile(idx.reshape(-1, 16).T, (8, 1)).astype(np.uint16)


def unstriped(offs):
    return offs[:16].T.reshape(-1).astype(np.int64)


def pack_weight(w):
    k, n = w.shape
    w = f64(np.asarray(w, np.float32).astype(ml_dtypes.bfloat16)).reshape(k // 32, 32, n)
    amax = np.abs(w).max(1)
    byte = np.clip(np.where(amax > 0, np.frexp(amax)[1] - 1 + 127 - 7, 1), 1, 254)
    scaled = (w * np.exp2(127.0 - byte)[:, None, :]).reshape(k, n).astype(np.float32)
    words = np.ascontiguousarray(scaled.reshape(k // 512, 128, 4, n).transpose(0, 1, 3, 2)).astype(ml_dtypes.float8_e4m3fn).view(np.uint8)
    return words, np.ascontiguousarray(byte.astype(np.uint8).reshape(k // 512, 16, n))


def unpack_weight(words, scales):
    g, p, n, _ = words.shape
    vals = np.ascontiguousarray(words).view(ml_dtypes.float8_e4m3fn).astype(np.float64) * np.repeat(np.exp2(scales.astype(np.float64) - 127.0), 8, axis=1)[..., None]
    return vals.transpose(0, 1, 3, 2).reshape(g * 512, n)


def gelu(v):
    return 0.5 * v * (1.0 + np.tanh(np.sqrt(2.0 / np.pi) * (v + 0.044715 * v**3)))


K, T, S, V, H, N = 512, 1024, 512, 256, 512, 256


def setup_inputs():
    n = np.random.standard_normal
    s = mx_kscale(K)[:, None]
    u = mx_kscale(H)
    packed_w3 = pack_weight(n((H, N)) / np.sqrt(H) / u[:, None])
    return {
        "xT": (n((K, T)) * s).astype(np.float32),
        "w1": (n((K, H)) / np.sqrt(2 * K) / s * u).astype(np.float32),
        "w2": (n((K, H)) / np.sqrt(2 * K) / s * u).astype(np.float32),
        "w3_words": packed_w3[0],
        "w3_scales": packed_w3[1],
        "offs": striped(np.random.permutation(T)[:S]),
        "cen": striped(np.random.permutation(S)[:V]),
        "pos1": striped(np.random.permutation(S)[:V]),
        "pos2": striped(np.random.permutation(S)[:V]),
        "pos3": striped(np.random.permutation(S)[:V]),
    }


def reference(xT, w1, w2, w3_words, w3_scales, offs, cen, pos1, pos2, pos3):
    xq = mxq(f64(xT)[:, unstriped(offs)], 0, "e4m3")
    y = mxq(f64(w1), 0, "e4m3").T @ xq
    yc = y[:, unstriped(cen)]
    e = mxq(f64(w2), 0, "e4m3").T @ xq
    z = np.maximum(np.maximum(gelu(yc + e[:, unstriped(pos1)]), gelu(yc + e[:, unstriped(pos2)])), gelu(yc + e[:, unstriped(pos3)]))
    return unpack_weight(w3_words, w3_scales).T @ mxq(z, 0, "e4m3")

@@ -1,0 +1,189 @@
+from contextlib import ExitStack
+
+import concourse.mybir as mybir
+
+K, T, S, V, H, N = 512, 1024, 512, 256, 512, 256
+FLOPS = 2 * 2 * K * H * S + 2 * H * N * V
+
+F32 = mybir.dt.float32
+BF16 = mybir.dt.bfloat16
+I32 = mybir.dt.int32
+U32 = mybir.dt.uint32
+U16 = mybir.dt.uint16
+U8 = mybir.dt.uint8
+FP8X4 = mybir.dt.float8_e4m3fn_x4
+ADD = mybir.AluOpType.add
+MAX = mybir.AluOpType.max
+GELU = mybir.ActivationFunctionType.Gelu_apprx_tanh
+
+P = 128
+PACK = 4
+RUN = 4
+LIST_ROWS = 16
+
+
+def tile_picked_edgecv_gelu_e_kernel(
+    tc, xT, w1, w2, w3_words, w3_scales, offs, cen, pos1, pos2, pos3, out
+):
+    nc = tc.nc
+    with ExitStack() as ctx:
+        keep = ctx.enter_context(tc.tile_pool(name="keep", bufs=1))
+        psum = ctx.enter_context(tc.psum_pool(name="psum", bufs=1))
+
+        def sbuf(name, shape, dtype, tag=None):
+            return keep.tile(shape, dtype, name=name, tag=tag or name, align_bytes=64)
+
+        def load_list(name, src):
+            tile = keep.tile(list(src.shape), U16, name=name)
+            nc.sync.dma_start(tile[:], src)
+            return tile
+
+        def load_weight_half(name, w, half):
+            tile = sbuf(name, [P, PACK, H // 2], F32)
+            rows = w.rearrange("(p j) c -> p j c", j=PACK)
+            nc.sync.dma_start(tile[:], rows[:, :, half * (H // 2) : (half + 1) * (H // 2)])
+            return tile
+
+        warm_in = sbuf("warm_in", [P, 1], F32)
+        warm_out = sbuf("warm_out", [P, 1], F32)
+        nc.vector.memset(warm_in[:], 0.0)
+        nc.scalar.activation(warm_out[:], warm_in[:], GELU)
+
+        w3_bytes = sbuf("w3_bytes", [P, N], U8)
+        nc.vector.memset(w3_bytes[:].bitcast(I32), 0)
+
+        x_rows = xT.rearrange("(p j) t -> p j t", j=PACK)
+        x_planes = [sbuf(f"x_plane{j}", [P, T], F32) for j in range(PACK)]
+        nc.sync.dma_start(x_planes[0][:], x_rows[:, 0, :])
+        offs_sb = load_list("offs_sb", offs)
+        for j in range(1, PACK):
+            nc.sync.dma_start(x_planes[j][:], x_rows[:, j, :])
+        w1_raw = [load_weight_half(f"w1_raw{h}", w1, h) for h in range(2)]
+        cen_sb = load_list("cen_sb", cen)
+        w2_raw = [load_weight_half(f"w2_raw{h}", w2, h) for h in range(2)]
+        pos_sb = [load_list(f"pos_sb{d}", src) for d, src in enumerate((pos1, pos2, pos3))]
+        w3_codes = sbuf("w3_codes", [P, N], I32)
+        nc.sync.dma_start(w3_codes[:], w3_words[0].rearrange("p n t -> p (n t)").bitcast(I32))
+        for q in range(4):
+            nc.sync.dma_start(
+                w3_bytes[32 * q : 32 * q + 4, :].bitcast(I32), w3_scales[0, 4 * q : 4 * q + 4, :].bitcast(I32)
+            )
+
+        picked = sbuf("picked", [P, PACK, S], BF16)
+        x_woven = sbuf("x_woven", [P, S, PACK], BF16)
+        for j0, engine_copy in ((0, nc.scalar.copy), (2, nc.vector.tensor_copy)):
+            for j in (j0, j0 + 1):
+                nc.vector.tensor_copy(picked[:, j, :], x_planes[j][:].indirect(offs_sb[:]))
+            engine_copy(x_woven[:, :, j0 : j0 + 2], picked[:, j0 : j0 + 2, :].rearrange("p j s -> p s j"))
+        x_codes = sbuf("x_codes", [P, S], U32)
+        x_bytes = sbuf("x_bytes", [P, S], U8)
+        nc.vector.quantize_mx(x_codes[:].bitcast(FP8X4), x_bytes[:], x_woven[:].rearrange("p s j -> p (s j)"))
+
+        def round_weight_half(engine_copy, woven, raw, half, lo=0, hi=P // 2):
+            m0 = half * (P // 2)
+            engine_copy(
+                woven[:, :, m0 + lo : m0 + hi, :].rearrange("p t m j -> p m j t"),
+                raw[:, :, PACK * lo : PACK * hi].rearrange("p j (m t) -> p m j t", t=PACK),
+            )
+
+        def quantize_weight(codes, scale_bytes, woven, t0, t1):
+            nc.vector.quantize_mx(
+                codes[:, t0 * P : t1 * P].bitcast(FP8X4),
+                scale_bytes[:, t0 * P : t1 * P],
+                woven[:, t0:t1, :, :].rearrange("p t m j -> p (t m j)"),
+            )
+
+        def product(name, codes, scale_bytes, t):
+            bank = psum.tile([P, S], F32, name=f"{name}_bank{t}", tag=f"{name}_bank{t}")
+            nc.tensor.matmul_mx(
+                bank[:],
+                lhsT=codes[:, t * P : (t + 1) * P].bitcast(FP8X4),
+                lhsT_scale=scale_bytes[:, t * P : (t + 1) * P],
+                rhs=x_codes[:].bitcast(FP8X4),
+                rhs_scale=x_bytes[:],
+                start=True,
+                stop=True,
+            )
+            rows = sbuf(f"{name}_rows{t}", [P, S], F32)
+            nc.scalar.copy(rows[:], bank[:])
+            return rows
+
+        w1_woven = sbuf("w1_woven", [P, PACK, P, PACK], BF16)
+        w1_codes = sbuf("w1_codes", [P, H], U32)
+        w1_bytes = sbuf("w1_bytes", [P, H], U8)
+        round_weight_half(nc.scalar.copy, w1_woven, w1_raw[0], 0)
+        round_weight_half(nc.vector.tensor_copy, w1_woven, w1_raw[1], 1, 0, 32)
+        round_weight_half(nc.scalar.copy, w1_woven, w1_raw[1], 1, 32, 64)
+        for t0, t1 in ((0, 1), (1, 2), (2, 4)):
+            quantize_weight(w1_codes, w1_bytes, w1_woven, t0, t1)
+
+        w2_woven = sbuf("w2_woven", [P, PACK, P, PACK], BF16)
+        w2_codes = sbuf("w2_codes", [P, H], U32)
+        w2_bytes = sbuf("w2_bytes", [P, H], U8)
+        round_weight_half(nc.scalar.copy, w2_woven, w2_raw[0], 0)
+        round_weight_half(nc.vector.tensor_copy, w2_woven, w2_raw[1], 1)
+        quantize_weight(w2_codes, w2_bytes, w2_woven, 0, PACK)
+        y_rows = [product("y", w1_codes, w1_bytes, t) for t in range(PACK)]
+        e_rows = [product("e", w2_codes, w2_bytes, t) for t in range(PACK)]
+        centre = sbuf("centre", [P, PACK, V], F32, tag="w2_woven")
+        for t in range(PACK):
+            nc.vector.tensor_copy(centre[:, t, :], y_rows[t][:].indirect(cen_sb[:]))
+
+        edge = [sbuf(f"edge{d}", [P, PACK, V], F32) for d in range(2)]
+        edge.append(edge[0])
+        act = [sbuf(f"act{d}", [P, V, PACK], BF16) for d in range(3)]
+
+        def edges(d, lo, hi):
+            for t in range(PACK):
+                nc.vector.tensor_tensor(
+                    edge[d][:, t, lo:hi],
+                    e_rows[t][:].indirect(pos_sb[d][:, lo // LIST_ROWS : hi // LIST_ROWS]),
+                    centre[:, t, lo:hi],
+                    ADD,
+                )
+
+        def gelu(d, lo, hi):
+            nc.scalar.activation(
+                act[d][:, lo:hi, :].rearrange("p (c i) t -> p c t i", i=RUN),
+                edge[d][:, :, lo:hi].rearrange("p t (c i) -> p c t i", i=RUN),
+                GELU,
+            )
+
+        def flat(tile, lo, hi):
+            return tile[:, lo:hi, :].rearrange("p v t -> p (v t)")
+
+        best_two = sbuf("best_two", [P, V, PACK], BF16)
+        z = sbuf("z", [P, V, PACK], BF16)
+        z_codes = sbuf("z_codes", [P, V], U32)
+        z_bytes = sbuf("z_bytes", [P, V], U8)
+        out_rows = out.rearrange("(h p) v -> p h v", p=P)
+
+        halves = ((0, V // 2), (V // 2, V))
+        edges(0, 0, V)
+        edges(1, 0, V)
+        for lo, hi in halves:
+            gelu(0, lo, hi)
+        gelu(1, 0, V)
+        for lo, hi in halves:
+            edges(2, lo, hi)
+            gelu(2, lo, hi)
+        nc.vector.tensor_tensor(flat(best_two, 0, V), flat(act[0], 0, V), flat(act[1], 0, V), MAX)
+        for lo, hi in halves:
+            nc.vector.tensor_tensor(flat(z, lo, hi), flat(best_two, lo, hi), flat(act[2], lo, hi), MAX)
+        for lo, hi in halves:
+            nc.vector.quantize_mx(z_codes[:, lo:hi].bitcast(FP8X4), z_bytes[:, lo:hi], flat(z, lo, hi))
+        for g, (lo, hi) in enumerate(halves):
+            bank = psum.tile([P, N // P, hi - lo], F32, name=f"out_bank{g}", tag=f"y_bank{g}")
+            for h in range(N // P):
+                nc.tensor.matmul_mx(
+                    bank[:, h, :],
+                    lhsT=w3_codes[:, h * P : (h + 1) * P].bitcast(FP8X4),
+                    lhsT_scale=w3_bytes[:, h * P : (h + 1) * P],
+                    rhs=z_codes[:, lo:hi].bitcast(FP8X4),
+                    rhs_scale=z_bytes[:, lo:hi],
+                    start=True,
+                    stop=True,
+                )
+            staged = sbuf(f"staged{g}", [P, N // P, hi - lo], F32)
+            (nc.scalar.copy, nc.vector.tensor_copy)[g](staged[:], bank[:])
+            nc.sync.dma_start(out_rows[:, :, lo:hi], staged[:])

@@ -28,6 +28,7 @@ def tile_picked_edgecv_gelu_e_kernel(
     nc = tc.nc
     with ExitStack() as ctx:
         keep = ctx.enter_context(tc.tile_pool(name="keep", bufs=1))
+        reuse = ctx.enter_context(tc.tile_pool(name="reuse", bufs=1))
         psum = ctx.enter_context(tc.psum_pool(name="psum", bufs=1))
 
         def sbuf(name, shape, dtype, tag=None):
@@ -38,10 +39,8 @@ def tile_picked_edgecv_gelu_e_kernel(
             nc.sync.dma_start(tile[:], src)
             return tile
 
-        def load_weight_half(name, w, half):
-            tile = sbuf(name, [P, PACK, H // 2], F32)
-            rows = w.rearrange("(p j) c -> p j c", j=PACK)
-            nc.sync.dma_start(tile[:], rows[:, :, half * (H // 2) : (half + 1) * (H // 2)])
+        def load_weight(tile, w):
+            nc.sync.dma_start(tile[:], w.rearrange("(p j) c -> p j c", j=PACK))
             return tile
 
         warm_in = sbuf("warm_in", [P, 1], F32)
@@ -54,13 +53,12 @@ def tile_picked_edgecv_gelu_e_kernel(
 
         x_rows = xT.rearrange("(p j) t -> p j t", j=PACK)
         x_planes = [sbuf(f"x_plane{j}", [P, T], F32) for j in range(PACK)]
-        nc.sync.dma_start(x_planes[0][:], x_rows[:, 0, :])
         offs_sb = load_list("offs_sb", offs)
-        for j in range(1, PACK):
+        for j in range(PACK):
             nc.sync.dma_start(x_planes[j][:], x_rows[:, j, :])
-        w1_raw = [load_weight_half(f"w1_raw{h}", w1, h) for h in range(2)]
+        w1_raw = load_weight(sbuf("w1_raw", [P, PACK, H], F32), w1)
         cen_sb = load_list("cen_sb", cen)
-        w2_raw = [load_weight_half(f"w2_raw{h}", w2, h) for h in range(2)]
+        w2_raw = load_weight(reuse.tile([P, PACK, H], F32, name="w2_raw", offset=0), w2)
         pos_sb = [load_list(f"pos_sb{d}", src) for d, src in enumerate((pos1, pos2, pos3))]
         w3_codes = sbuf("w3_codes", [P, N], I32)
         nc.sync.dma_start(w3_codes[:], w3_words[0].rearrange("p n t -> p (n t)").bitcast(I32))
@@ -70,61 +68,62 @@ def tile_picked_edgecv_gelu_e_kernel(
             )
 
         picked = sbuf("picked", [P, PACK, S], BF16)
-        x_woven = sbuf("x_woven", [P, S, PACK], BF16)
-        for j0, engine_copy in ((0, nc.scalar.copy), (2, nc.vector.tensor_copy)):
+        xw1_woven = sbuf("xw1_woven", [P, (S + H) * PACK], BF16)
+        x_woven = xw1_woven[:, : S * PACK].rearrange("p (s j) -> p s j", j=PACK)
+        w1_woven = xw1_woven[:, S * PACK :].rearrange("p (t m j) -> p t m j", t=PACK, j=PACK)
+        split = 288
+        for j0 in (0, 2):
             for j in (j0, j0 + 1):
                 nc.vector.tensor_copy(picked[:, j, :], x_planes[j][:].indirect(offs_sb[:]))
-            engine_copy(x_woven[:, :, j0 : j0 + 2], picked[:, j0 : j0 + 2, :].rearrange("p j s -> p s j"))
-        x_codes = sbuf("x_codes", [P, S], U32)
-        x_bytes = sbuf("x_bytes", [P, S], U8)
-        nc.vector.quantize_mx(x_codes[:].bitcast(FP8X4), x_bytes[:], x_woven[:].rearrange("p s j -> p (s j)"))
-
-        def round_weight_half(engine_copy, woven, raw, half, lo=0, hi=P // 2):
-            m0 = half * (P // 2)
-            engine_copy(
-                woven[:, :, m0 + lo : m0 + hi, :].rearrange("p t m j -> p m j t"),
-                raw[:, :, PACK * lo : PACK * hi].rearrange("p j (m t) -> p m j t", t=PACK),
+            nc.scalar.copy(
+                x_woven[:, split:, j0 : j0 + 2], picked[:, j0 : j0 + 2, split:].rearrange("p j s -> p s j")
             )
+        nc.vector.tensor_copy(
+            x_woven[:, :split, :].rearrange("p (c i) j -> p c j i", i=RUN),
+            picked[:, :, :split].rearrange("p j (c i) -> p c j i", i=RUN),
+        )
 
-        def quantize_weight(codes, scale_bytes, woven, t0, t1):
-            nc.vector.quantize_mx(
-                codes[:, t0 * P : t1 * P].bitcast(FP8X4),
-                scale_bytes[:, t0 * P : t1 * P],
-                woven[:, t0:t1, :, :].rearrange("p t m j -> p (t m j)"),
-            )
+        def round_weight(woven, raw, split):
+            for engine_copy, lo, hi in ((nc.vector.tensor_copy, 0, split), (nc.scalar.copy, split, P)):
+                engine_copy(
+                    woven[:, :, lo:hi, :].rearrange("p t m j -> p m j t"),
+                    raw[:, :, PACK * lo : PACK * hi].rearrange("p j (m t) -> p m j t", t=PACK),
+                )
 
-        def product(name, codes, scale_bytes, t):
-            bank = psum.tile([P, S], F32, name=f"{name}_bank{t}", tag=f"{name}_bank{t}")
+        def quantize(name, woven):
+            width = woven.shape[1] // PACK
+            codes = sbuf(f"{name}_codes", [P, width], U32)
+            scale_bytes = sbuf(f"{name}_bytes", [P, width], U8)
+            nc.vector.quantize_mx(codes[:].bitcast(FP8X4), scale_bytes[:], woven)
+            return codes, scale_bytes
+
+        def multiply(bank, lhs, lhs_cols, rhs, rhs_cols):
             nc.tensor.matmul_mx(
-                bank[:],
-                lhsT=codes[:, t * P : (t + 1) * P].bitcast(FP8X4),
-                lhsT_scale=scale_bytes[:, t * P : (t + 1) * P],
-                rhs=x_codes[:].bitcast(FP8X4),
-                rhs_scale=x_bytes[:],
+                bank,
+                lhsT=lhs[0][:, lhs_cols].bitcast(FP8X4),
+                lhsT_scale=lhs[1][:, lhs_cols],
+                rhs=rhs[0][:, rhs_cols].bitcast(FP8X4),
+                rhs_scale=rhs[1][:, rhs_cols],
                 start=True,
                 stop=True,
             )
-            rows = sbuf(f"{name}_rows{t}", [P, S], F32)
+
+        def product(name, weight, first_col, t, rows):
+            bank = psum.tile([P, S], F32, name=f"{name}_bank{t}", tag=f"{name}_bank{t}")
+            multiply(bank[:], weight, slice(first_col + t * P, first_col + (t + 1) * P), xw1_mx, slice(0, S))
             nc.scalar.copy(rows[:], bank[:])
             return rows
 
-        w1_woven = sbuf("w1_woven", [P, PACK, P, PACK], BF16)
-        w1_codes = sbuf("w1_codes", [P, H], U32)
-        w1_bytes = sbuf("w1_bytes", [P, H], U8)
-        round_weight_half(nc.scalar.copy, w1_woven, w1_raw[0], 0)
-        round_weight_half(nc.vector.tensor_copy, w1_woven, w1_raw[1], 1, 0, 32)
-        round_weight_half(nc.scalar.copy, w1_woven, w1_raw[1], 1, 32, 64)
-        for t0, t1 in ((0, 1), (1, 2), (2, 4)):
-            quantize_weight(w1_codes, w1_bytes, w1_woven, t0, t1)
-
+        round_weight(w1_woven, w1_raw, 76)
+        xw1_mx = quantize("xw1", xw1_woven[:])
         w2_woven = sbuf("w2_woven", [P, PACK, P, PACK], BF16)
-        w2_codes = sbuf("w2_codes", [P, H], U32)
-        w2_bytes = sbuf("w2_bytes", [P, H], U8)
-        round_weight_half(nc.scalar.copy, w2_woven, w2_raw[0], 0)
-        round_weight_half(nc.vector.tensor_copy, w2_woven, w2_raw[1], 1)
-        quantize_weight(w2_codes, w2_bytes, w2_woven, 0, PACK)
-        y_rows = [product("y", w1_codes, w1_bytes, t) for t in range(PACK)]
-        e_rows = [product("e", w2_codes, w2_bytes, t) for t in range(PACK)]
+        round_weight(w2_woven, w2_raw, 76)
+        w2_mx = quantize("w2", w2_woven[:].rearrange("p t m j -> p (t m j)"))
+        y_rows = [
+            product("y", xw1_mx, S, t, reuse.tile([P, S], F32, name=f"y_rows{t}", offset=t * S * 4))
+            for t in range(PACK)
+        ]
+        e_rows = [product("e", w2_mx, 0, t, sbuf(f"e_rows{t}", [P, S], F32)) for t in range(PACK)]
         centre = sbuf("centre", [P, PACK, V], F32, tag="w2_woven")
         for t in range(PACK):
             nc.vector.tensor_copy(centre[:, t, :], y_rows[t][:].indirect(cen_sb[:]))
@@ -154,8 +153,6 @@ def tile_picked_edgecv_gelu_e_kernel(
 
         best_two = sbuf("best_two", [P, V, PACK], BF16)
         z = sbuf("z", [P, V, PACK], BF16)
-        z_codes = sbuf("z_codes", [P, V], U32)
-        z_bytes = sbuf("z_bytes", [P, V], U8)
         out_rows = out.rearrange("(h p) v -> p h v", p=P)
 
         halves = ((0, V // 2), (V // 2, V))
@@ -170,20 +167,11 @@ def tile_picked_edgecv_gelu_e_kernel(
         nc.vector.tensor_tensor(flat(best_two, 0, V), flat(act[0], 0, V), flat(act[1], 0, V), MAX)
         for lo, hi in halves:
             nc.vector.tensor_tensor(flat(z, lo, hi), flat(best_two, lo, hi), flat(act[2], lo, hi), MAX)
-        for lo, hi in halves:
-            nc.vector.quantize_mx(z_codes[:, lo:hi].bitcast(FP8X4), z_bytes[:, lo:hi], flat(z, lo, hi))
+        z_mx = [quantize(f"z{g}", flat(z, lo, hi)) for g, (lo, hi) in enumerate(halves)]
         for g, (lo, hi) in enumerate(halves):
-            bank = psum.tile([P, N // P, hi - lo], F32, name=f"out_bank{g}", tag=f"y_bank{g}")
-            for h in range(N // P):
-                nc.tensor.matmul_mx(
-                    bank[:, h, :],
-                    lhsT=w3_codes[:, h * P : (h + 1) * P].bitcast(FP8X4),
-                    lhsT_scale=w3_bytes[:, h * P : (h + 1) * P],
-                    rhs=z_codes[:, lo:hi].bitcast(FP8X4),
-                    rhs_scale=z_bytes[:, lo:hi],
-                    start=True,
-                    stop=True,
-                )
             staged = sbuf(f"staged{g}", [P, N // P, hi - lo], F32)
-            (nc.scalar.copy, nc.vector.tensor_copy)[g](staged[:], bank[:])
+            for h, engine_copy in enumerate((nc.scalar.copy, nc.vector.tensor_copy)):
+                bank = psum.tile([P, hi - lo], F32, name=f"out_bank{g}{h}", tag=f"y_bank{2 * g + h}")
+                multiply(bank[:], (w3_codes, w3_bytes), slice(h * P, (h + 1) * P), z_mx[g], slice(0, hi - lo))
+                engine_copy(staged[:, h, :], bank[:])
             nc.sync.dma_start(out_rows[:, :, lo:hi], staged[:])

@@ -43,10 +43,6 @@ def tile_picked_edgecv_gelu_e_kernel(
             nc.sync.dma_start(tile[:], w.rearrange("(p j) c -> p j c", j=PACK))
             return tile
 
-        warm_in = sbuf("warm_in", [P, 1], F32)
-        warm_out = sbuf("warm_out", [P, 1], F32)
-        nc.vector.memset(warm_in[:], 0.0)
-        nc.scalar.activation(warm_out[:], warm_in[:], GELU)
 
         w3_bytes = sbuf("w3_bytes", [P, N], U8)
         nc.vector.memset(w3_bytes[:].bitcast(I32), 0)
@@ -68,33 +64,41 @@ def tile_picked_edgecv_gelu_e_kernel(
             )
 
         picked = sbuf("picked", [P, PACK, S], BF16)
+        half = H // 2 * PACK
         xw1_woven = sbuf("xw1_woven", [P, (S + H) * PACK], BF16)
-        x_woven = xw1_woven[:, : S * PACK].rearrange("p (s j) -> p s j", j=PACK)
-        w1_woven = xw1_woven[:, S * PACK :].rearrange("p (t m j) -> p t m j", t=PACK, j=PACK)
-        split = 288
-        for j0 in (0, 2):
-            for j in (j0, j0 + 1):
-                nc.vector.tensor_copy(picked[:, j, :], x_planes[j][:].indirect(offs_sb[:]))
-            nc.scalar.copy(
-                x_woven[:, split:, j0 : j0 + 2], picked[:, j0 : j0 + 2, split:].rearrange("p j s -> p s j")
+        x_woven = xw1_woven[:, half : half + S * PACK].rearrange("p (s j) -> p s j", j=PACK)
+        w1_woven = (xw1_woven[:, :half], xw1_woven[:, half + S * PACK :])
+        share = 64
+        for j in range(PACK - 1):
+            nc.vector.tensor_copy(picked[:, j, :], x_planes[j][:].indirect(offs_sb[:]))
+        shares = ((nc.vector.tensor_copy, share, S), (nc.scalar.copy, 0, share))
+        for engine_copy, lo, hi in shares:
+            nc.vector.tensor_copy(
+                picked[:, PACK - 1, lo:hi],
+                x_planes[PACK - 1][:].indirect(offs_sb[:, lo // LIST_ROWS : hi // LIST_ROWS]),
             )
-        nc.vector.tensor_copy(
-            x_woven[:, :split, :].rearrange("p (c i) j -> p c j i", i=RUN),
-            picked[:, :, :split].rearrange("p j (c i) -> p c j i", i=RUN),
-        )
+        for engine_copy, lo, hi in shares:
+            engine_copy(
+                x_woven[:, lo:hi, :].rearrange("p (c i) j -> p c j i", i=RUN),
+                picked[:, :, lo:hi].rearrange("p j (c i) -> p c j i", i=RUN),
+            )
 
-        def round_weight(woven, raw, split):
-            for engine_copy, lo, hi in ((nc.vector.tensor_copy, 0, split), (nc.scalar.copy, split, P)):
+        def round_weight(woven, raw):
+            for u, engine_copy in enumerate((nc.scalar.copy, nc.vector.tensor_copy)):
                 engine_copy(
-                    woven[:, :, lo:hi, :].rearrange("p t m j -> p m j t"),
-                    raw[:, :, PACK * lo : PACK * hi].rearrange("p j (m t) -> p m j t", t=PACK),
+                    woven[u].rearrange("p (t m j) -> p m j t", t=2, j=PACK),
+                    raw[:].rearrange("p j (m t) -> p m j t", t=PACK)[:, :, :, 2 * u : 2 * u + 2],
                 )
 
-        def quantize(name, woven):
+        def quantize(name, woven, pieces=1):
             width = woven.shape[1] // PACK
             codes = sbuf(f"{name}_codes", [P, width], U32)
             scale_bytes = sbuf(f"{name}_bytes", [P, width], U8)
-            nc.vector.quantize_mx(codes[:].bitcast(FP8X4), scale_bytes[:], woven)
+            for lo in range(0, width, width // pieces):
+                hi = lo + width // pieces
+                nc.vector.quantize_mx(
+                    codes[:, lo:hi].bitcast(FP8X4), scale_bytes[:, lo:hi], woven[:, PACK * lo : PACK * hi]
+                )
             return codes, scale_bytes
 
         def multiply(bank, lhs, lhs_cols, rhs, rhs_cols):
@@ -108,22 +112,25 @@ def tile_picked_edgecv_gelu_e_kernel(
                 stop=True,
             )
 
-        def product(name, weight, first_col, t, rows):
-            bank = psum.tile([P, S], F32, name=f"{name}_bank{t}", tag=f"{name}_bank{t}")
-            multiply(bank[:], weight, slice(first_col + t * P, first_col + (t + 1) * P), xw1_mx, slice(0, S))
-            nc.scalar.copy(rows[:], bank[:])
+        def product(weight, first_col, rows, pieces):
+            for tag, lo, hi in pieces:
+                bank = psum.tile([P, hi - lo], F32, name=tag, tag=tag)
+                multiply(bank[:], weight, slice(first_col, first_col + P), xw1_mx, slice(H // 2 + lo, H // 2 + hi))
+                nc.scalar.copy(rows[:, lo:hi], bank[:])
             return rows
 
-        round_weight(w1_woven, w1_raw, 76)
-        xw1_mx = quantize("xw1", xw1_woven[:])
-        w2_woven = sbuf("w2_woven", [P, PACK, P, PACK], BF16)
-        round_weight(w2_woven, w2_raw, 76)
-        w2_mx = quantize("w2", w2_woven[:].rearrange("p t m j -> p (t m j)"))
-        y_rows = [
-            product("y", xw1_mx, S, t, reuse.tile([P, S], F32, name=f"y_rows{t}", offset=t * S * 4))
-            for t in range(PACK)
-        ]
-        e_rows = [product("e", w2_mx, 0, t, sbuf(f"e_rows{t}", [P, S], F32)) for t in range(PACK)]
+        round_weight(w1_woven, w1_raw)
+        xw1_mx = quantize("xw1", xw1_woven[:], pieces=2)
+        w2_woven = sbuf("w2_woven", [P, H * PACK], BF16)
+        round_weight((w2_woven[:, :half], w2_woven[:, half:]), w2_raw)
+        w2_mx = quantize("w2", w2_woven[:])
+        y_rows = [reuse.tile([P, S], F32, name=f"y_rows{t}", offset=t * S * 4) for t in range(PACK)]
+        e_rows = [sbuf(f"e_rows{t}", [P, S], F32) for t in range(PACK)]
+        product(xw1_mx, 0, y_rows[0], (("bank0", 0, S // 2), ("bank1", S // 2, S)))
+        for t in range(1, PACK):
+            product(xw1_mx, t * P + (t // 2) * S, y_rows[t], ((f"bank{t + 1}", 0, S),))
+        for t in range(PACK):
+            product(w2_mx, t * P, e_rows[t], ((f"bank{(t + 5) % 8}", 0, S),))
         centre = sbuf("centre", [P, PACK, V], F32, tag="w2_woven")
         for t in range(PACK):
             nc.vector.tensor_copy(centre[:, t, :], y_rows[t][:].indirect(cen_sb[:]))
@@ -153,7 +160,6 @@ def tile_picked_edgecv_gelu_e_kernel(
 
         best_two = sbuf("best_two", [P, V, PACK], BF16)
         z = sbuf("z", [P, V, PACK], BF16)
-        out_rows = out.rearrange("(h p) v -> p h v", p=P)
 
         halves = ((0, V // 2), (V // 2, V))
         edges(0, 0, V)
@@ -169,9 +175,9 @@ def tile_picked_edgecv_gelu_e_kernel(
             nc.vector.tensor_tensor(flat(z, lo, hi), flat(best_two, lo, hi), flat(act[2], lo, hi), MAX)
         z_mx = [quantize(f"z{g}", flat(z, lo, hi)) for g, (lo, hi) in enumerate(halves)]
         for g, (lo, hi) in enumerate(halves):
-            staged = sbuf(f"staged{g}", [P, N // P, hi - lo], F32)
-            for h, engine_copy in enumerate((nc.scalar.copy, nc.vector.tensor_copy)):
-                bank = psum.tile([P, hi - lo], F32, name=f"out_bank{g}{h}", tag=f"y_bank{2 * g + h}")
+            for h, (engine_copy, queue) in enumerate(((nc.scalar.copy, nc.scalar), (nc.vector.tensor_copy, nc.sync))):
+                bank = psum.tile([P, hi - lo], F32, name=f"out_bank{g}{h}", tag=f"bank{1 + 2 * g + h}")
                 multiply(bank[:], (w3_codes, w3_bytes), slice(h * P, (h + 1) * P), z_mx[g], slice(0, hi - lo))
-                engine_copy(staged[:, h, :], bank[:])
-            nc.sync.dma_start(out_rows[:, :, lo:hi], staged[:])
+                staged = sbuf(f"staged{g}{h}", [P, hi - lo], F32)
+                engine_copy(staged[:], bank[:])
+                queue.dma_start(out[h * P : (h + 1) * P, lo:hi], staged[:])

@@ -84,10 +84,15 @@ def tile_picked_edgecv_gelu_e_kernel(
             )
 
         def round_weight(woven, raw):
-            for u, engine_copy in enumerate((nc.scalar.copy, nc.vector.tensor_copy)):
+            cut = 40
+            for engine_copy, u, lo, hi in (
+                (nc.vector.tensor_copy, 0, 0, cut),
+                (nc.scalar.copy, 0, cut, P),
+                (nc.vector.tensor_copy, 1, 0, P),
+            ):
                 engine_copy(
-                    woven[u].rearrange("p (t m j) -> p m j t", t=2, j=PACK),
-                    raw[:].rearrange("p j (m t) -> p m j t", t=PACK)[:, :, :, 2 * u : 2 * u + 2],
+                    woven[u].rearrange("p (t m j) -> p m j t", t=2, j=PACK)[:, lo:hi],
+                    raw[:].rearrange("p j (m t) -> p m j t", t=PACK)[:, lo:hi, :, 2 * u : 2 * u + 2],
                 )
 
         def quantize(name, woven, pieces=1):
@@ -123,7 +128,7 @@ def tile_picked_edgecv_gelu_e_kernel(
         xw1_mx = quantize("xw1", xw1_woven[:], pieces=2)
         w2_woven = sbuf("w2_woven", [P, H * PACK], BF16)
         round_weight((w2_woven[:, :half], w2_woven[:, half:]), w2_raw)
-        w2_mx = quantize("w2", w2_woven[:])
+        w2_mx = quantize("w2", w2_woven[:], pieces=2)
         y_rows = [reuse.tile([P, S], F32, name=f"y_rows{t}", offset=t * S * 4) for t in range(PACK)]
         e_rows = [sbuf(f"e_rows{t}", [P, S], F32) for t in range(PACK)]
         product(xw1_mx, 0, y_rows[0], (("bank0", 0, S // 2), ("bank1", S // 2, S)))

@@ -18,8 +18,15 @@ GELU = mybir.ActivationFunctionType.Gelu_apprx_tanh
 
 P = 128
 PACK = 4
+PAIR = 2
 RUN = 4
 LIST_ROWS = 16
+QUADRANT = 32
+BANKS = 8
+F32_BYTES = 4
+
+SCALAR_POINTS = 64
+VECTOR_COLUMNS = 40
 
 
 def tile_picked_edgecv_gelu_e_kernel(
@@ -31,8 +38,8 @@ def tile_picked_edgecv_gelu_e_kernel(
         reuse = ctx.enter_context(tc.tile_pool(name="reuse", bufs=1))
         psum = ctx.enter_context(tc.psum_pool(name="psum", bufs=1))
 
-        def sbuf(name, shape, dtype, tag=None):
-            return keep.tile(shape, dtype, name=name, tag=tag or name, align_bytes=64)
+        def sbuf(name, shape, dtype):
+            return keep.tile(shape, dtype, name=name, tag=name, align_bytes=64)
 
         def load_list(name, src):
             tile = keep.tile(list(src.shape), U16, name=name)
@@ -43,59 +50,60 @@ def tile_picked_edgecv_gelu_e_kernel(
             nc.sync.dma_start(tile[:], w.rearrange("(p j) c -> p j c", j=PACK))
             return tile
 
-
         w3_bytes = sbuf("w3_bytes", [P, N], U8)
         nc.vector.memset(w3_bytes[:].bitcast(I32), 0)
 
         x_rows = xT.rearrange("(p j) t -> p j t", j=PACK)
         x_planes = [sbuf(f"x_plane{j}", [P, T], F32) for j in range(PACK)]
+        nc.sync.dma_start(x_planes[0][:], x_rows[:, 0, :])
         offs_sb = load_list("offs_sb", offs)
-        for j in range(PACK):
+        for j in range(1, PACK):
             nc.sync.dma_start(x_planes[j][:], x_rows[:, j, :])
         w1_raw = load_weight(sbuf("w1_raw", [P, PACK, H], F32), w1)
-        cen_sb = load_list("cen_sb", cen)
         w2_raw = load_weight(reuse.tile([P, PACK, H], F32, name="w2_raw", offset=0), w2)
+        cen_sb = load_list("cen_sb", cen)
         pos_sb = [load_list(f"pos_sb{d}", src) for d, src in enumerate((pos1, pos2, pos3))]
         w3_codes = sbuf("w3_codes", [P, N], I32)
         nc.sync.dma_start(w3_codes[:], w3_words[0].rearrange("p n t -> p (n t)").bitcast(I32))
-        for q in range(4):
+        for q in range(P // QUADRANT):
             nc.sync.dma_start(
-                w3_bytes[32 * q : 32 * q + 4, :].bitcast(I32), w3_scales[0, 4 * q : 4 * q + 4, :].bitcast(I32)
+                w3_bytes[QUADRANT * q : QUADRANT * q + 4, :].bitcast(I32),
+                w3_scales[0, 4 * q : 4 * q + 4, :].bitcast(I32),
             )
 
-        picked = sbuf("picked", [P, PACK, S], BF16)
-        half = H // 2 * PACK
+        pair_width = PAIR * P * PACK
         xw1_woven = sbuf("xw1_woven", [P, (S + H) * PACK], BF16)
-        x_woven = xw1_woven[:, half : half + S * PACK].rearrange("p (s j) -> p s j", j=PACK)
-        w1_woven = (xw1_woven[:, :half], xw1_woven[:, half + S * PACK :])
-        share = 64
+        x_woven = xw1_woven[:, pair_width : pair_width + S * PACK].rearrange("p (s j) -> p s j", j=PACK)
+        w1_pairs = (xw1_woven[:, :pair_width], xw1_woven[:, pair_width + S * PACK :])
+        x_first = PAIR * P
+
+        picked = sbuf("picked", [P, PACK, S], BF16)
         for j in range(PACK - 1):
             nc.vector.tensor_copy(picked[:, j, :], x_planes[j][:].indirect(offs_sb[:]))
-        shares = ((nc.vector.tensor_copy, share, S), (nc.scalar.copy, 0, share))
-        for engine_copy, lo, hi in shares:
+        point_shares = ((nc.vector.tensor_copy, SCALAR_POINTS, S), (nc.scalar.copy, 0, SCALAR_POINTS))
+        for engine_copy, lo, hi in point_shares:
             nc.vector.tensor_copy(
                 picked[:, PACK - 1, lo:hi],
                 x_planes[PACK - 1][:].indirect(offs_sb[:, lo // LIST_ROWS : hi // LIST_ROWS]),
             )
-        for engine_copy, lo, hi in shares:
+        for engine_copy, lo, hi in point_shares:
             engine_copy(
                 x_woven[:, lo:hi, :].rearrange("p (c i) j -> p c j i", i=RUN),
                 picked[:, :, lo:hi].rearrange("p j (c i) -> p c j i", i=RUN),
             )
 
-        def round_weight(woven, raw):
-            cut = 40
+        def round_weight(pairs, raw):
             for engine_copy, u, lo, hi in (
-                (nc.vector.tensor_copy, 0, 0, cut),
-                (nc.scalar.copy, 0, cut, P),
+                (nc.vector.tensor_copy, 0, 0, VECTOR_COLUMNS),
+                (nc.scalar.copy, 0, VECTOR_COLUMNS, P),
                 (nc.vector.tensor_copy, 1, 0, P),
             ):
                 engine_copy(
-                    woven[u].rearrange("p (t m j) -> p m j t", t=2, j=PACK)[:, lo:hi],
-                    raw[:].rearrange("p j (m t) -> p m j t", t=PACK)[:, lo:hi, :, 2 * u : 2 * u + 2],
+                    pairs[u].rearrange("p (t m j) -> p m j t", t=PAIR, j=PACK)[:, lo:hi],
+                    raw[:].rearrange("p j (m t) -> p m j t", t=PACK)[:, lo:hi, :, PAIR * u : PAIR * (u + 1)],
                 )
 
-        def quantize(name, woven, pieces=1):
+        def quantize(name, woven, pieces):
             width = woven.shape[1] // PACK
             codes = sbuf(f"{name}_codes", [P, width], U32)
             scale_bytes = sbuf(f"{name}_bytes", [P, width], U8)
@@ -117,26 +125,27 @@ def tile_picked_edgecv_gelu_e_kernel(
                 stop=True,
             )
 
-        def product(weight, first_col, rows, pieces):
-            for tag, lo, hi in pieces:
-                bank = psum.tile([P, hi - lo], F32, name=tag, tag=tag)
-                multiply(bank[:], weight, slice(first_col, first_col + P), xw1_mx, slice(H // 2 + lo, H // 2 + hi))
+        def hidden_rows(weight, first_col, rows, pieces):
+            for bank_no, lo, hi in pieces:
+                bank = psum.tile([P, hi - lo], F32, name=f"bank{bank_no}", tag=f"bank{bank_no}")
+                multiply(bank[:], weight, slice(first_col, first_col + P), xw1_mx, slice(x_first + lo, x_first + hi))
                 nc.scalar.copy(rows[:, lo:hi], bank[:])
-            return rows
 
-        round_weight(w1_woven, w1_raw)
+        round_weight(w1_pairs, w1_raw)
         xw1_mx = quantize("xw1", xw1_woven[:], pieces=2)
         w2_woven = sbuf("w2_woven", [P, H * PACK], BF16)
-        round_weight((w2_woven[:, :half], w2_woven[:, half:]), w2_raw)
+        round_weight((w2_woven[:, :pair_width], w2_woven[:, pair_width:]), w2_raw)
         w2_mx = quantize("w2", w2_woven[:], pieces=2)
-        y_rows = [reuse.tile([P, S], F32, name=f"y_rows{t}", offset=t * S * 4) for t in range(PACK)]
+
+        y_rows = [reuse.tile([P, S], F32, name=f"y_rows{t}", offset=t * S * F32_BYTES) for t in range(PACK)]
         e_rows = [sbuf(f"e_rows{t}", [P, S], F32) for t in range(PACK)]
-        product(xw1_mx, 0, y_rows[0], (("bank0", 0, S // 2), ("bank1", S // 2, S)))
+        hidden_rows(xw1_mx, 0, y_rows[0], ((0, 0, S // 2), (1, S // 2, S)))
         for t in range(1, PACK):
-            product(xw1_mx, t * P + (t // 2) * S, y_rows[t], ((f"bank{t + 1}", 0, S),))
+            hidden_rows(xw1_mx, t * P + (t // PAIR) * S, y_rows[t], ((1 + t, 0, S),))
         for t in range(PACK):
-            product(w2_mx, t * P, e_rows[t], ((f"bank{(t + 5) % 8}", 0, S),))
-        centre = sbuf("centre", [P, PACK, V], F32, tag="w2_woven")
+            hidden_rows(w2_mx, t * P, e_rows[t], (((1 + PACK + t) % BANKS, 0, S),))
+
+        centre = sbuf("centre", [P, PACK, V], F32)
         for t in range(PACK):
             nc.vector.tensor_copy(centre[:, t, :], y_rows[t][:].indirect(cen_sb[:]))
 
@@ -144,7 +153,7 @@ def tile_picked_edgecv_gelu_e_kernel(
         edge.append(edge[0])
         act = [sbuf(f"act{d}", [P, V, PACK], BF16) for d in range(3)]
 
-        def edges(d, lo, hi):
+        def edge_sums(d, lo, hi):
             for t in range(PACK):
                 nc.vector.tensor_tensor(
                     edge[d][:, t, lo:hi],
@@ -167,21 +176,23 @@ def tile_picked_edgecv_gelu_e_kernel(
         z = sbuf("z", [P, V, PACK], BF16)
 
         halves = ((0, V // 2), (V // 2, V))
-        edges(0, 0, V)
-        edges(1, 0, V)
+        edge_sums(0, 0, V)
+        edge_sums(1, 0, V)
         for lo, hi in halves:
             gelu(0, lo, hi)
         gelu(1, 0, V)
         for lo, hi in halves:
-            edges(2, lo, hi)
+            edge_sums(2, lo, hi)
             gelu(2, lo, hi)
         nc.vector.tensor_tensor(flat(best_two, 0, V), flat(act[0], 0, V), flat(act[1], 0, V), MAX)
         for lo, hi in halves:
             nc.vector.tensor_tensor(flat(z, lo, hi), flat(best_two, lo, hi), flat(act[2], lo, hi), MAX)
-        z_mx = [quantize(f"z{g}", flat(z, lo, hi)) for g, (lo, hi) in enumerate(halves)]
+        z_mx = [quantize(f"z{g}", flat(z, lo, hi), pieces=1) for g, (lo, hi) in enumerate(halves)]
+
+        ways_out = ((nc.scalar.copy, nc.scalar), (nc.vector.tensor_copy, nc.sync))
         for g, (lo, hi) in enumerate(halves):
-            for h, (engine_copy, queue) in enumerate(((nc.scalar.copy, nc.scalar), (nc.vector.tensor_copy, nc.sync))):
-                bank = psum.tile([P, hi - lo], F32, name=f"out_bank{g}{h}", tag=f"bank{1 + 2 * g + h}")
+            for h, (engine_copy, queue) in enumerate(ways_out):
+                bank = psum.tile([P, hi - lo], F32, name=f"out_bank{g}{h}", tag=f"bank{1 + len(ways_out) * g + h}")
                 multiply(bank[:], (w3_codes, w3_bytes), slice(h * P, (h + 1) * P), z_mx[g], slice(0, hi - lo))
                 staged = sbuf(f"staged{g}{h}", [P, hi - lo], F32)
                 engine_copy(staged[:], bank[:])

@@ -14,6 +14,7 @@ U8 = mybir.dt.uint8
 FP8X4 = mybir.dt.float8_e4m3fn_x4
 ADD = mybir.AluOpType.add
 MAX = mybir.AluOpType.max
+COPY = mybir.ActivationFunctionType.Copy
 GELU = mybir.ActivationFunctionType.Gelu_apprx_tanh
 
 P = 128
@@ -25,8 +26,10 @@ QUADRANT = 32
 BANKS = 8
 F32_BYTES = 4
 
-SCALAR_POINTS = 64
+SCALAR_POINTS = 256
 VECTOR_COLUMNS = 40
+OVERLAP = 16
+FIRST_GELU = 64
 
 
 def tile_picked_edgecv_gelu_e_kernel(
@@ -53,6 +56,10 @@ def tile_picked_edgecv_gelu_e_kernel(
         w3_bytes = sbuf("w3_bytes", [P, N], U8)
         nc.vector.memset(w3_bytes[:].bitcast(I32), 0)
 
+        warm = sbuf("warm", [P, 8], F32)
+        nc.vector.memset(warm[:], 0.0)
+        nc.scalar.activation(warm[:, 4:5], warm[:, 0:1], GELU)
+
         x_rows = xT.rearrange("(p j) t -> p j t", j=PACK)
         x_planes = [sbuf(f"x_plane{j}", [P, T], F32) for j in range(PACK)]
         nc.sync.dma_start(x_planes[0][:], x_rows[:, 0, :])
@@ -60,7 +67,8 @@ def tile_picked_edgecv_gelu_e_kernel(
         for j in range(1, PACK):
             nc.sync.dma_start(x_planes[j][:], x_rows[:, j, :])
         w1_raw = load_weight(sbuf("w1_raw", [P, PACK, H], F32), w1)
-        w2_raw = load_weight(reuse.tile([P, PACK, H], F32, name="w2_raw", offset=0), w2)
+        w2_early = load_weight(reuse.tile([P, PACK, H // 2], F32, name="w2_early", offset=0), w2[:, : H // 2])
+        w2_late = load_weight(sbuf("w2_late", [P, PACK, H // 2], F32), w2[:, H // 2 :])
         cen_sb = load_list("cen_sb", cen)
         pos_sb = [load_list(f"pos_sb{d}", src) for d, src in enumerate((pos1, pos2, pos3))]
         w3_codes = sbuf("w3_codes", [P, N], I32)
@@ -78,9 +86,12 @@ def tile_picked_edgecv_gelu_e_kernel(
         x_first = PAIR * P
 
         picked = sbuf("picked", [P, PACK, S], BF16)
-        for j in range(PACK - 1):
-            nc.vector.tensor_copy(picked[:, j, :], x_planes[j][:].indirect(offs_sb[:]))
-        point_shares = ((nc.vector.tensor_copy, SCALAR_POINTS, S), (nc.scalar.copy, 0, SCALAR_POINTS))
+        for j in range(PAIR):
+            rounded = sbuf(f"x_rounded{j}", [P, T], BF16)
+            nc.vector.tensor_copy(rounded[:], x_planes[j][:])
+            nc.scalar.activation(picked[:, j, :], rounded[:].indirect(offs_sb[:]), COPY)
+        nc.vector.tensor_copy(picked[:, PAIR, :], x_planes[PAIR][:].indirect(offs_sb[:]))
+        point_shares = ((nc.scalar.copy, 0, SCALAR_POINTS), (nc.vector.tensor_copy, SCALAR_POINTS, S))
         for engine_copy, lo, hi in point_shares:
             nc.vector.tensor_copy(
                 picked[:, PACK - 1, lo:hi],
@@ -103,9 +114,12 @@ def tile_picked_edgecv_gelu_e_kernel(
                     raw[:].rearrange("p j (m t) -> p m j t", t=PACK)[:, lo:hi, :, PAIR * u : PAIR * (u + 1)],
                 )
 
-        def quantize(name, woven, pieces):
+        def quantize(name, woven, pieces, offset=None):
             width = woven.shape[1] // PACK
-            codes = sbuf(f"{name}_codes", [P, width], U32)
+            if offset is None:
+                codes = sbuf(f"{name}_codes", [P, width], U32)
+            else:
+                codes = reuse.tile([P, width], U32, name=f"{name}_codes", offset=offset, align_bytes=64)
             scale_bytes = sbuf(f"{name}_bytes", [P, width], U8)
             for lo in range(0, width, width // pieces):
                 hi = lo + width // pieces
@@ -134,10 +148,16 @@ def tile_picked_edgecv_gelu_e_kernel(
         round_weight(w1_pairs, w1_raw)
         xw1_mx = quantize("xw1", xw1_woven[:], pieces=2)
         w2_woven = sbuf("w2_woven", [P, H * PACK], BF16)
-        round_weight((w2_woven[:, :pair_width], w2_woven[:, pair_width:]), w2_raw)
+        for engine_copy, raw, lo in ((nc.scalar.copy, w2_early, 0), (nc.vector.tensor_copy, w2_late, P // 2)):
+            for u in range(2):
+                engine_copy(
+                    w2_woven[:, u * pair_width : (u + 1) * pair_width].rearrange("p (t m j) -> p m j t", t=PAIR, j=PACK)[:, lo : lo + P // 2],
+                    raw[:].rearrange("p j (m t) -> p m j t", t=PACK)[:, :, :, PAIR * u : PAIR * (u + 1)],
+                )
         w2_mx = quantize("w2", w2_woven[:], pieces=2)
 
-        y_rows = [reuse.tile([P, S], F32, name=f"y_rows{t}", offset=t * S * F32_BYTES) for t in range(PACK)]
+        y_rows = [reuse.tile([P, S], F32, name=f"y_rows{t}", offset=t * S * F32_BYTES) for t in range(PAIR)]
+        y_rows.extend(sbuf(f"y_rows{t}", [P, S], F32) for t in range(PAIR, PACK))
         e_rows = [sbuf(f"e_rows{t}", [P, S], F32) for t in range(PACK)]
         hidden_rows(xw1_mx, 0, y_rows[0], ((0, 0, S // 2), (1, S // 2, S)))
         for t in range(1, PACK):
@@ -149,14 +169,22 @@ def tile_picked_edgecv_gelu_e_kernel(
         for t in range(PACK):
             nc.vector.tensor_copy(centre[:, t, :], y_rows[t][:].indirect(cen_sb[:]))
 
-        edge = [sbuf(f"edge{d}", [P, PACK, V], F32) for d in range(2)]
-        edge.append(edge[0])
+        shared = sbuf("edge02", [P, PACK, 2 * V - OVERLAP], F32)
+        first_col = V - OVERLAP
+        edge0 = shared[:, :, first_col : first_col + V]
+        edge1 = sbuf("edge1", [P, PACK, V], F32)
+
+        def edge(d, lo, hi):
+            if d < 2:
+                return (edge0, edge1[:])[d][:, :, lo:hi]
+            return shared[:, :, lo:hi]
+
         act = [sbuf(f"act{d}", [P, V, PACK], BF16) for d in range(3)]
 
-        def edge_sums(d, lo, hi):
-            for t in range(PACK):
+        def edge_sums(d, lo, hi, tiles=range(PACK)):
+            for t in tiles:
                 nc.vector.tensor_tensor(
-                    edge[d][:, t, lo:hi],
+                    edge(d, lo, hi)[:, t, :],
                     e_rows[t][:].indirect(pos_sb[d][:, lo // LIST_ROWS : hi // LIST_ROWS]),
                     centre[:, t, lo:hi],
                     ADD,
@@ -165,29 +193,35 @@ def tile_picked_edgecv_gelu_e_kernel(
         def gelu(d, lo, hi):
             nc.scalar.activation(
                 act[d][:, lo:hi, :].rearrange("p (c i) t -> p c t i", i=RUN),
-                edge[d][:, :, lo:hi].rearrange("p t (c i) -> p c t i", i=RUN),
+                edge(d, lo, hi).rearrange("p t (c i) -> p c t i", i=RUN),
                 GELU,
             )
 
         def flat(tile, lo, hi):
             return tile[:, lo:hi, :].rearrange("p v t -> p (v t)")
 
-        best_two = sbuf("best_two", [P, V, PACK], BF16)
+        spare = PACK * H * F32_BYTES
+        best_two = [
+            sbuf("best_two0", [P, V // 2 * PACK], BF16),
+            reuse.tile([P, V // 2 * PACK], BF16, name="best_two1", offset=spare, align_bytes=64),
+        ]
         z = sbuf("z", [P, V, PACK], BF16)
 
         halves = ((0, V // 2), (V // 2, V))
         edge_sums(0, 0, V)
         edge_sums(1, 0, V)
-        for lo, hi in halves:
-            gelu(0, lo, hi)
+        gelu(0, 0, FIRST_GELU)
+        gelu(0, FIRST_GELU, V)
         gelu(1, 0, V)
+        edge_sums(2, 0, V, range(PAIR))
         for lo, hi in halves:
-            edge_sums(2, lo, hi)
+            edge_sums(2, lo, hi, range(PAIR, PACK))
             gelu(2, lo, hi)
-        nc.vector.tensor_tensor(flat(best_two, 0, V), flat(act[0], 0, V), flat(act[1], 0, V), MAX)
-        for lo, hi in halves:
-            nc.vector.tensor_tensor(flat(z, lo, hi), flat(best_two, lo, hi), flat(act[2], lo, hi), MAX)
-        z_mx = [quantize(f"z{g}", flat(z, lo, hi), pieces=1) for g, (lo, hi) in enumerate(halves)]
+        for g, (lo, hi) in enumerate(halves):
+            nc.vector.tensor_tensor(best_two[g][:], flat(act[0], lo, hi), flat(act[1], lo, hi), MAX)
+        for g, (lo, hi) in enumerate(halves):
+            nc.vector.tensor_tensor(flat(z, lo, hi), best_two[g][:], flat(act[2], lo, hi), MAX)
+        z_mx = [quantize("z0", flat(z, *halves[0]), pieces=1, offset=spare), quantize("z1", flat(z, *halves[1]), pieces=1)]
 
         ways_out = ((nc.scalar.copy, nc.scalar), (nc.vector.tensor_copy, nc.sync))
         for g, (lo, hi) in enumerate(halves):

@@ -14,7 +14,6 @@ U8 = mybir.dt.uint8
 FP8X4 = mybir.dt.float8_e4m3fn_x4
 ADD = mybir.AluOpType.add
 MAX = mybir.AluOpType.max
-COPY = mybir.ActivationFunctionType.Copy
 GELU = mybir.ActivationFunctionType.Gelu_apprx_tanh
 
 P = 128
@@ -56,10 +55,6 @@ def tile_picked_edgecv_gelu_e_kernel(
         w3_bytes = sbuf("w3_bytes", [P, N], U8)
         nc.vector.memset(w3_bytes[:].bitcast(I32), 0)
 
-        warm = sbuf("warm", [P, 8], F32)
-        nc.vector.memset(warm[:], 0.0)
-        nc.scalar.activation(warm[:, 4:5], warm[:, 0:1], GELU)
-
         x_rows = xT.rearrange("(p j) t -> p j t", j=PACK)
         x_planes = [sbuf(f"x_plane{j}", [P, T], F32) for j in range(PACK)]
         nc.sync.dma_start(x_planes[0][:], x_rows[:, 0, :])
@@ -86,12 +81,9 @@ def tile_picked_edgecv_gelu_e_kernel(
         x_first = PAIR * P
 
         picked = sbuf("picked", [P, PACK, S], BF16)
-        for j in range(PAIR):
-            rounded = sbuf(f"x_rounded{j}", [P, T], BF16)
-            nc.vector.tensor_copy(rounded[:], x_planes[j][:])
-            nc.scalar.activation(picked[:, j, :], rounded[:].indirect(offs_sb[:]), COPY)
-        nc.vector.tensor_copy(picked[:, PAIR, :], x_planes[PAIR][:].indirect(offs_sb[:]))
-        point_shares = ((nc.scalar.copy, 0, SCALAR_POINTS), (nc.vector.tensor_copy, SCALAR_POINTS, S))
+        for j in range(PACK - 1):
+            nc.vector.tensor_copy(picked[:, j, :], x_planes[j][:].indirect(offs_sb[:]))
+        point_shares = ((nc.scalar.copy, 0, 224), (nc.vector.tensor_copy, 224, 448), (nc.scalar.copy, 448, S))
         for engine_copy, lo, hi in point_shares:
             nc.vector.tensor_copy(
                 picked[:, PACK - 1, lo:hi],

@@ -62,8 +62,7 @@ def tile_picked_edgecv_gelu_e_kernel(
         for j in range(1, PACK):
             nc.sync.dma_start(x_planes[j][:], x_rows[:, j, :])
         w1_raw = load_weight(sbuf("w1_raw", [P, PACK, H], F32), w1)
-        w2_early = load_weight(reuse.tile([P, PACK, H // 2], F32, name="w2_early", offset=0), w2[:, : H // 2])
-        w2_late = load_weight(sbuf("w2_late", [P, PACK, H // 2], F32), w2[:, H // 2 :])
+        w2_raw = load_weight(reuse.tile([P, PACK, H], F32, name="w2_raw", offset=0), w2)
         cen_sb = load_list("cen_sb", cen)
         pos_sb = [load_list(f"pos_sb{d}", src) for d, src in enumerate((pos1, pos2, pos3))]
         w3_codes = sbuf("w3_codes", [P, N], I32)
@@ -140,22 +139,15 @@ def tile_picked_edgecv_gelu_e_kernel(
         round_weight(w1_pairs, w1_raw)
         xw1_mx = quantize("xw1", xw1_woven[:], pieces=2)
         w2_woven = sbuf("w2_woven", [P, H * PACK], BF16)
-        for engine_copy, raw, lo in ((nc.scalar.copy, w2_early, 0), (nc.vector.tensor_copy, w2_late, P // 2)):
-            for u in range(2):
-                engine_copy(
-                    w2_woven[:, u * pair_width : (u + 1) * pair_width].rearrange("p (t m j) -> p m j t", t=PAIR, j=PACK)[:, lo : lo + P // 2],
-                    raw[:].rearrange("p j (m t) -> p m j t", t=PACK)[:, :, :, PAIR * u : PAIR * (u + 1)],
-                )
+        round_weight((w2_woven[:, :pair_width], w2_woven[:, pair_width:]), w2_raw)
         w2_mx = quantize("w2", w2_woven[:], pieces=2)
 
-        y_rows = [reuse.tile([P, S], F32, name=f"y_rows{t}", offset=t * S * F32_BYTES) for t in range(PAIR)]
-        y_rows.extend(sbuf(f"y_rows{t}", [P, S], F32) for t in range(PAIR, PACK))
+        y_rows = [reuse.tile([P, S], F32, name=f"y_rows{t}", offset=t * S * F32_BYTES) for t in range(PACK)]
         e_rows = [sbuf(f"e_rows{t}", [P, S], F32) for t in range(PACK)]
-        hidden_rows(xw1_mx, 0, y_rows[0], ((0, 0, S // 2), (1, S // 2, S)))
-        for t in range(1, PACK):
-            hidden_rows(xw1_mx, t * P + (t // PAIR) * S, y_rows[t], ((1 + t, 0, S),))
         for t in range(PACK):
-            hidden_rows(w2_mx, t * P, e_rows[t], (((1 + PACK + t) % BANKS, 0, S),))
+            hidden_rows(xw1_mx, t * P + (t // PAIR) * S, y_rows[t], ((t, 0, S),))
+        for t in range(PACK):
+            hidden_rows(w2_mx, t * P, e_rows[t], ((PACK + t, 0, S),))
 
         centre = sbuf("centre", [P, PACK, V], F32)
         for t in range(PACK):

@@ -22,11 +22,12 @@ PAIR = 2
 RUN = 4
 LIST_ROWS = 16
 QUADRANT = 32
-BANKS = 8
-F32_BYTES = 4
 
-SCALAR_POINTS = 256
-VECTOR_COLUMNS = 40
+SCALAR_FIRST_POINTS = 224
+SCALAR_LAST_POINTS = 64
+W1_VECTOR_COLUMNS = 40
+W2_VECTOR_COLUMNS = 92
+
 OVERLAP = 16
 FIRST_GELU = 64
 
@@ -48,9 +49,8 @@ def tile_picked_edgecv_gelu_e_kernel(
             nc.sync.dma_start(tile[:], src)
             return tile
 
-        def load_weight(tile, w):
-            nc.sync.dma_start(tile[:], w.rearrange("(p j) c -> p j c", j=PACK))
-            return tile
+        def load_weight(raw, w):
+            nc.sync.dma_start(raw, w.rearrange("(p j) c -> p j c", j=PACK))
 
         w3_bytes = sbuf("w3_bytes", [P, N], U8)
         nc.vector.memset(w3_bytes[:].bitcast(I32), 0)
@@ -61,8 +61,12 @@ def tile_picked_edgecv_gelu_e_kernel(
         offs_sb = load_list("offs_sb", offs)
         for j in range(1, PACK):
             nc.sync.dma_start(x_planes[j][:], x_rows[:, j, :])
-        w1_raw = load_weight(sbuf("w1_raw", [P, PACK, H], F32), w1)
-        w2_raw = load_weight(reuse.tile([P, PACK, H], F32, name="w2_raw", offset=0), w2)
+        w1_tile = sbuf("w1_raw", [P, PACK, H], F32)
+        w1_raw = w1_tile[:]
+        load_weight(w1_raw, w1)
+        w2_then_y = sbuf("w2_then_y", [P, PACK * H + S - OVERLAP], F32)
+        w2_raw = w2_then_y[:, : PACK * H].rearrange("p (j c) -> p j c", j=PACK)
+        load_weight(w2_raw, w2)
         cen_sb = load_list("cen_sb", cen)
         pos_sb = [load_list(f"pos_sb{d}", src) for d, src in enumerate((pos1, pos2, pos3))]
         w3_codes = sbuf("w3_codes", [P, N], I32)
@@ -82,7 +86,11 @@ def tile_picked_edgecv_gelu_e_kernel(
         picked = sbuf("picked", [P, PACK, S], BF16)
         for j in range(PACK - 1):
             nc.vector.tensor_copy(picked[:, j, :], x_planes[j][:].indirect(offs_sb[:]))
-        point_shares = ((nc.scalar.copy, 0, 224), (nc.vector.tensor_copy, 224, 448), (nc.scalar.copy, 448, S))
+        point_shares = (
+            (nc.scalar.copy, 0, SCALAR_FIRST_POINTS),
+            (nc.vector.tensor_copy, SCALAR_FIRST_POINTS, S - SCALAR_LAST_POINTS),
+            (nc.scalar.copy, S - SCALAR_LAST_POINTS, S),
+        )
         for engine_copy, lo, hi in point_shares:
             nc.vector.tensor_copy(
                 picked[:, PACK - 1, lo:hi],
@@ -94,23 +102,15 @@ def tile_picked_edgecv_gelu_e_kernel(
                 picked[:, :, lo:hi].rearrange("p j (c i) -> p c j i", i=RUN),
             )
 
-        def round_weight(pairs, raw):
-            for engine_copy, u, lo, hi in (
-                (nc.vector.tensor_copy, 0, 0, VECTOR_COLUMNS),
-                (nc.scalar.copy, 0, VECTOR_COLUMNS, P),
-                (nc.vector.tensor_copy, 1, 0, P),
-            ):
+        def round_weight(pairs, raw, shares):
+            for engine_copy, u, lo, hi in shares:
                 engine_copy(
                     pairs[u].rearrange("p (t m j) -> p m j t", t=PAIR, j=PACK)[:, lo:hi],
-                    raw[:].rearrange("p j (m t) -> p m j t", t=PACK)[:, lo:hi, :, PAIR * u : PAIR * (u + 1)],
+                    raw.rearrange("p j (m t) -> p m j t", t=PACK)[:, lo:hi, :, PAIR * u : PAIR * (u + 1)],
                 )
 
-        def quantize(name, woven, pieces, offset=None):
+        def quantize(name, woven, pieces, codes):
             width = woven.shape[1] // PACK
-            if offset is None:
-                codes = sbuf(f"{name}_codes", [P, width], U32)
-            else:
-                codes = reuse.tile([P, width], U32, name=f"{name}_codes", offset=offset, align_bytes=64)
             scale_bytes = sbuf(f"{name}_bytes", [P, width], U8)
             for lo in range(0, width, width // pieces):
                 hi = lo + width // pieces
@@ -130,45 +130,55 @@ def tile_picked_edgecv_gelu_e_kernel(
                 stop=True,
             )
 
-        def hidden_rows(weight, first_col, rows, pieces):
-            for bank_no, lo, hi in pieces:
-                bank = psum.tile([P, hi - lo], F32, name=f"bank{bank_no}", tag=f"bank{bank_no}")
-                multiply(bank[:], weight, slice(first_col, first_col + P), xw1_mx, slice(x_first + lo, x_first + hi))
-                nc.scalar.copy(rows[:, lo:hi], bank[:])
+        def hidden_rows(weight, first_col, rows, bank_no):
+            bank = psum.tile([P, S], F32, name=f"bank{bank_no}", tag=f"bank{bank_no}")
+            multiply(bank[:], weight, slice(first_col, first_col + P), xw1_mx, slice(x_first, x_first + S))
+            nc.scalar.copy(rows, bank[:])
 
-        round_weight(w1_pairs, w1_raw)
-        xw1_mx = quantize("xw1", xw1_woven[:], pieces=2)
+        round_weight(
+            w1_pairs,
+            w1_raw,
+            (
+                (nc.vector.tensor_copy, 0, 0, W1_VECTOR_COLUMNS),
+                (nc.scalar.copy, 0, W1_VECTOR_COLUMNS, P),
+                (nc.vector.tensor_copy, 1, 0, P),
+            ),
+        )
+        xw1_mx = quantize("xw1", xw1_woven[:], 2, sbuf("xw1_codes", [P, S + H], U32))
         w2_woven = sbuf("w2_woven", [P, H * PACK], BF16)
-        round_weight((w2_woven[:, :pair_width], w2_woven[:, pair_width:]), w2_raw)
-        w2_mx = quantize("w2", w2_woven[:], pieces=2)
+        round_weight(
+            (w2_woven[:, :pair_width], w2_woven[:, pair_width:]),
+            w2_raw,
+            (
+                (nc.vector.tensor_copy, 0, 0, W2_VECTOR_COLUMNS),
+                (nc.scalar.copy, 0, W2_VECTOR_COLUMNS, P),
+                (nc.vector.tensor_copy, 1, 0, W2_VECTOR_COLUMNS),
+                (nc.scalar.copy, 1, W2_VECTOR_COLUMNS, P),
+            ),
+        )
+        w2_mx = quantize("w2", w2_woven[:], 2, sbuf("w2_codes", [P, H], U32))
 
-        y_rows = [reuse.tile([P, S], F32, name=f"y_rows{t}", offset=t * S * F32_BYTES) for t in range(PACK)]
+        y_first = (PACK * H - OVERLAP, 0, S, 2 * S)
+        y_rows = [w2_then_y[:, first : first + S] for first in y_first]
         e_rows = [sbuf(f"e_rows{t}", [P, S], F32) for t in range(PACK)]
         for t in range(PACK):
-            hidden_rows(xw1_mx, t * P + (t // PAIR) * S, y_rows[t], ((t, 0, S),))
+            hidden_rows(xw1_mx, t * P + (t // PAIR) * S, y_rows[t], t)
         for t in range(PACK):
-            hidden_rows(w2_mx, t * P, e_rows[t], ((PACK + t, 0, S),))
+            hidden_rows(w2_mx, t * P, e_rows[t][:], PACK + t)
 
         centre = sbuf("centre", [P, PACK, V], F32)
         for t in range(PACK):
-            nc.vector.tensor_copy(centre[:, t, :], y_rows[t][:].indirect(cen_sb[:]))
+            nc.vector.tensor_copy(centre[:, t, :], y_rows[t].indirect(cen_sb[:]))
 
-        shared = sbuf("edge02", [P, PACK, 2 * V - OVERLAP], F32)
-        first_col = V - OVERLAP
-        edge0 = shared[:, :, first_col : first_col + V]
-        edge1 = sbuf("edge1", [P, PACK, V], F32)
-
-        def edge(d, lo, hi):
-            if d < 2:
-                return (edge0, edge1[:])[d][:, :, lo:hi]
-            return shared[:, :, lo:hi]
-
+        edges_2_0 = sbuf("edges_2_0", [P, PACK, 2 * V - OVERLAP], F32)
+        edges_1 = sbuf("edges_1", [P, PACK, V], F32)
+        edge = (edges_2_0[:, :, V - OVERLAP :], edges_1[:], edges_2_0[:, :, :V])
         act = [sbuf(f"act{d}", [P, V, PACK], BF16) for d in range(3)]
 
-        def edge_sums(d, lo, hi, tiles=range(PACK)):
+        def edge_sums(d, lo, hi, tiles):
             for t in tiles:
                 nc.vector.tensor_tensor(
-                    edge(d, lo, hi)[:, t, :],
+                    edge[d][:, t, lo:hi],
                     e_rows[t][:].indirect(pos_sb[d][:, lo // LIST_ROWS : hi // LIST_ROWS]),
                     centre[:, t, lo:hi],
                     ADD,
@@ -177,23 +187,16 @@ def tile_picked_edgecv_gelu_e_kernel(
         def gelu(d, lo, hi):
             nc.scalar.activation(
                 act[d][:, lo:hi, :].rearrange("p (c i) t -> p c t i", i=RUN),
-                edge(d, lo, hi).rearrange("p t (c i) -> p c t i", i=RUN),
+                edge[d][:, :, lo:hi].rearrange("p t (c i) -> p c t i", i=RUN),
                 GELU,
             )
 
         def flat(tile, lo, hi):
             return tile[:, lo:hi, :].rearrange("p v t -> p (v t)")
 
-        spare = PACK * H * F32_BYTES
-        best_two = [
-            sbuf("best_two0", [P, V // 2 * PACK], BF16),
-            reuse.tile([P, V // 2 * PACK], BF16, name="best_two1", offset=spare, align_bytes=64),
-        ]
-        z = sbuf("z", [P, V, PACK], BF16)
-
         halves = ((0, V // 2), (V // 2, V))
-        edge_sums(0, 0, V)
-        edge_sums(1, 0, V)
+        edge_sums(0, 0, V, range(PACK))
+        edge_sums(1, 0, V, range(PACK))
         gelu(0, 0, FIRST_GELU)
         gelu(0, FIRST_GELU, V)
         gelu(1, 0, V)
@@ -201,11 +204,21 @@ def tile_picked_edgecv_gelu_e_kernel(
         for lo, hi in halves:
             edge_sums(2, lo, hi, range(PAIR, PACK))
             gelu(2, lo, hi)
+
+        best_two = [
+            sbuf("best_two0", [P, V // 2 * PACK], BF16),
+            reuse.tile([P, V // 2 * PACK], BF16, name="best_two1", offset=0, align_bytes=64),
+        ]
+        z = sbuf("z", [P, V, PACK], BF16)
         for g, (lo, hi) in enumerate(halves):
             nc.vector.tensor_tensor(best_two[g][:], flat(act[0], lo, hi), flat(act[1], lo, hi), MAX)
         for g, (lo, hi) in enumerate(halves):
             nc.vector.tensor_tensor(flat(z, lo, hi), best_two[g][:], flat(act[2], lo, hi), MAX)
-        z_mx = [quantize("z0", flat(z, *halves[0]), pieces=1, offset=spare), quantize("z1", flat(z, *halves[1]), pieces=1)]
+        z_codes = [
+            reuse.tile([P, V // 2], U32, name="z0_codes", offset=0, align_bytes=64),
+            sbuf("z1_codes", [P, V // 2], U32),
+        ]
+        z_mx = [quantize(f"z{g}", flat(z, lo, hi), 1, z_codes[g]) for g, (lo, hi) in enumerate(halves)]
 
         ways_out = ((nc.scalar.copy, nc.scalar), (nc.vector.tensor_copy, nc.sync))
         for g, (lo, hi) in enumerate(halves):

@@ -29,7 +29,7 @@ W1_VECTOR_COLUMNS = 40
 W2_VECTOR_COLUMNS = 92
 
 OVERLAP = 16
-FIRST_GELU = 64
+END_GELU = 64
 
 
 def tile_picked_edgecv_gelu_e_kernel(
@@ -54,6 +54,10 @@ def tile_picked_edgecv_gelu_e_kernel(
 
         w3_bytes = sbuf("w3_bytes", [P, N], U8)
         nc.vector.memset(w3_bytes[:].bitcast(I32), 0)
+
+        warm = sbuf("warm", [P, 8], F32)
+        nc.vector.memset(warm[:], 0.0)
+        nc.scalar.activation(warm[:, 4:5], warm[:, 0:1], GELU)
 
         x_rows = xT.rearrange("(p j) t -> p j t", j=PACK)
         x_planes = [sbuf(f"x_plane{j}", [P, T], F32) for j in range(PACK)]
@@ -170,9 +174,12 @@ def tile_picked_edgecv_gelu_e_kernel(
         for t in range(PACK):
             nc.vector.tensor_copy(centre[:, t, :], y_rows[t].indirect(cen_sb[:]))
 
-        edges_2_0 = sbuf("edges_2_0", [P, PACK, 2 * V - OVERLAP], F32)
-        edges_1 = sbuf("edges_1", [P, PACK, V], F32)
-        edge = (edges_2_0[:, :, V - OVERLAP :], edges_1[:], edges_2_0[:, :, :V])
+        edges = sbuf("edges", [P, 2 * PACK - 1, 3 * V - 2 * OVERLAP], F32)
+        edge = (
+            edges[:, :PACK, V - OVERLAP : 2 * V - OVERLAP],
+            edges[:, PACK - 1 :, 2 * (V - OVERLAP) :],
+            edges[:, :PACK, :V],
+        )
         act = [sbuf(f"act{d}", [P, V, PACK], BF16) for d in range(3)]
 
         def edge_sums(d, lo, hi, tiles):
@@ -196,9 +203,11 @@ def tile_picked_edgecv_gelu_e_kernel(
 
         halves = ((0, V // 2), (V // 2, V))
         edge_sums(0, 0, V, range(PACK))
-        edge_sums(1, 0, V, range(PACK))
-        gelu(0, 0, FIRST_GELU)
-        gelu(0, FIRST_GELU, V)
+        edge_sums(1, 0, V, range(1, PACK))
+        gelu(0, V - END_GELU, V)
+        edge_sums(1, 0, V, (0,))
+        gelu(0, 0, END_GELU)
+        gelu(0, END_GELU, V - END_GELU)
         gelu(1, 0, V)
         edge_sums(2, 0, V, range(PAIR))
         for lo, hi in halves:

@@ -25,11 +25,11 @@ QUADRANT = 32
 
 SCALAR_FIRST_POINTS = 224
 SCALAR_LAST_POINTS = 64
-W1_VECTOR_COLUMNS = 40
-W2_VECTOR_COLUMNS = 92
+W1_VECTOR_COLUMNS = 76
+W2_VECTOR_COLUMNS = 102
 
 OVERLAP = 16
-END_GELU = 64
+END_GELU = 32
 
 
 def tile_picked_edgecv_gelu_e_kernel(
@@ -174,10 +174,10 @@ def tile_picked_edgecv_gelu_e_kernel(
         for t in range(PACK):
             nc.vector.tensor_copy(centre[:, t, :], y_rows[t].indirect(cen_sb[:]))
 
-        edges = sbuf("edges", [P, 2 * PACK - 1, 3 * V - 2 * OVERLAP], F32)
+        edges = sbuf("edges", [P, PACK + 1, 3 * V - 2 * OVERLAP], F32)
         edge = (
             edges[:, :PACK, V - OVERLAP : 2 * V - OVERLAP],
-            edges[:, PACK - 1 :, 2 * (V - OVERLAP) :],
+            edges[:, 1:, 2 * (V - OVERLAP) :],
             edges[:, :PACK, :V],
         )
         act = [sbuf(f"act{d}", [P, V, PACK], BF16) for d in range(3)]
@@ -203,11 +203,10 @@ def tile_picked_edgecv_gelu_e_kernel(
 
         halves = ((0, V // 2), (V // 2, V))
         edge_sums(0, 0, V, range(PACK))
-        edge_sums(1, 0, V, range(1, PACK))
+        edge_sums(1, 0, V, (PACK - 1,))
         gelu(0, V - END_GELU, V)
-        edge_sums(1, 0, V, (0,))
-        gelu(0, 0, END_GELU)
-        gelu(0, END_GELU, V - END_GELU)
+        edge_sums(1, 0, V, range(PACK - 1))
+        gelu(0, 0, V - END_GELU)
         gelu(1, 0, V)
         edge_sums(2, 0, V, range(PAIR))
         for lo, hi in halves:

@@ -14,6 +14,7 @@ U8 = mybir.dt.uint8
 FP8X4 = mybir.dt.float8_e4m3fn_x4
 ADD = mybir.AluOpType.add
 MAX = mybir.AluOpType.max
+COPY = mybir.ActivationFunctionType.Copy
 GELU = mybir.ActivationFunctionType.Gelu_apprx_tanh
 
 P = 128
@@ -23,10 +24,11 @@ RUN = 4
 LIST_ROWS = 16
 QUADRANT = 32
 
-SCALAR_FIRST_POINTS = 224
+SCALAR_PLANES = 2
+SCALAR_FIRST_POINTS = 192
 SCALAR_LAST_POINTS = 64
-W1_VECTOR_COLUMNS = 76
-W2_VECTOR_COLUMNS = 102
+W1_VECTOR_COLUMNS = 40
+W2_VECTOR_COLUMNS = 96
 
 OVERLAP = 16
 END_GELU = 32
@@ -82,13 +84,17 @@ def tile_picked_edgecv_gelu_e_kernel(
             )
 
         pair_width = PAIR * P * PACK
-        xw1_woven = sbuf("xw1_woven", [P, (S + H) * PACK], BF16)
-        x_woven = xw1_woven[:, pair_width : pair_width + S * PACK].rearrange("p (s j) -> p s j", j=PACK)
-        w1_pairs = (xw1_woven[:, :pair_width], xw1_woven[:, pair_width + S * PACK :])
-        x_first = PAIR * P
+        x_woven_tile = sbuf("x_woven", [P, S * PACK], BF16)
+        x_woven = x_woven_tile[:].rearrange("p (s j) -> p s j", j=PACK)
+        w1_woven = sbuf("w1_woven", [P, H * PACK], BF16)
+        w1_pairs = (w1_woven[:, :pair_width], w1_woven[:, pair_width:])
 
         picked = sbuf("picked", [P, PACK, S], BF16)
-        for j in range(PACK - 1):
+        for j in range(SCALAR_PLANES):
+            rounded = sbuf(f"x_rounded{j}", [P, T], BF16)
+            nc.vector.tensor_copy(rounded[:], x_planes[j][:])
+            nc.scalar.activation(picked[:, j, :], rounded[:].indirect(offs_sb[:]), COPY)
+        for j in range(SCALAR_PLANES, PACK - 1):
             nc.vector.tensor_copy(picked[:, j, :], x_planes[j][:].indirect(offs_sb[:]))
         point_shares = (
             (nc.scalar.copy, 0, SCALAR_FIRST_POINTS),
@@ -100,7 +106,13 @@ def tile_picked_edgecv_gelu_e_kernel(
                 picked[:, PACK - 1, lo:hi],
                 x_planes[PACK - 1][:].indirect(offs_sb[:, lo // LIST_ROWS : hi // LIST_ROWS]),
             )
-        for engine_copy, lo, hi in point_shares:
+        weave_shares = (
+            point_shares[0],
+            (nc.vector.tensor_copy, SCALAR_FIRST_POINTS, S // 2),
+            (nc.vector.tensor_copy, S // 2, S - SCALAR_LAST_POINTS),
+            point_shares[2],
+        )
+        for engine_copy, lo, hi in weave_shares:
             engine_copy(
                 x_woven[:, lo:hi, :].rearrange("p (c i) j -> p c j i", i=RUN),
                 picked[:, :, lo:hi].rearrange("p j (c i) -> p c j i", i=RUN),
@@ -136,29 +148,32 @@ def tile_picked_edgecv_gelu_e_kernel(
 
         def hidden_rows(weight, first_col, rows, bank_no):
             bank = psum.tile([P, S], F32, name=f"bank{bank_no}", tag=f"bank{bank_no}")
-            multiply(bank[:], weight, slice(first_col, first_col + P), xw1_mx, slice(x_first, x_first + S))
+            multiply(bank[:], weight, slice(first_col, first_col + P), x_mx, slice(0, S))
             nc.scalar.copy(rows, bank[:])
 
+        x_mx = quantize("x", x_woven_tile[:], 2, sbuf("x_codes", [P, S], U32))
         round_weight(
             w1_pairs,
             w1_raw,
             (
-                (nc.vector.tensor_copy, 0, 0, W1_VECTOR_COLUMNS),
-                (nc.scalar.copy, 0, W1_VECTOR_COLUMNS, P),
-                (nc.vector.tensor_copy, 1, 0, P),
+                (nc.vector.tensor_copy, 0, 0, P),
+                (nc.scalar.copy, 1, W1_VECTOR_COLUMNS, P),
+                (nc.vector.tensor_copy, 1, 0, W1_VECTOR_COLUMNS),
             ),
         )
-        xw1_mx = quantize("xw1", xw1_woven[:], 2, sbuf("xw1_codes", [P, S + H], U32))
+        w1_mx = quantize("w1", w1_woven[:], 2, sbuf("w1_codes", [P, H], U32))
         w2_woven = sbuf("w2_woven", [P, H * PACK], BF16)
         round_weight(
             (w2_woven[:, :pair_width], w2_woven[:, pair_width:]),
             w2_raw,
             (
                 (nc.vector.tensor_copy, 0, 0, W2_VECTOR_COLUMNS),
-                (nc.scalar.copy, 0, W2_VECTOR_COLUMNS, P),
                 (nc.vector.tensor_copy, 1, 0, W2_VECTOR_COLUMNS),
-                (nc.scalar.copy, 1, W2_VECTOR_COLUMNS, P),
             ),
+        )
+        nc.scalar.copy(
+            w2_woven[:].rearrange("p (t m j) -> p m j t", t=PACK, j=PACK)[:, W2_VECTOR_COLUMNS:],
+            w2_raw.rearrange("p j (m t) -> p m j t", t=PACK)[:, W2_VECTOR_COLUMNS:],
         )
         w2_mx = quantize("w2", w2_woven[:], 2, sbuf("w2_codes", [P, H], U32))
 
@@ -166,7 +181,7 @@ def tile_picked_edgecv_gelu_e_kernel(
         y_rows = [w2_then_y[:, first : first + S] for first in y_first]
         e_rows = [sbuf(f"e_rows{t}", [P, S], F32) for t in range(PACK)]
         for t in range(PACK):
-            hidden_rows(xw1_mx, t * P + (t // PAIR) * S, y_rows[t], t)
+            hidden_rows(w1_mx, t * P, y_rows[t], t)
         for t in range(PACK):
             hidden_rows(w2_mx, t * P, e_rows[t][:], PACK + t)
 

@@ -28,7 +28,7 @@ SCALAR_PLANES = 2
 SCALAR_FIRST_POINTS = 192
 SCALAR_LAST_POINTS = 64
 W1_VECTOR_COLUMNS = 40
-W2_VECTOR_COLUMNS = 96
+W2_VECTOR_COLUMNS = 100
 
 OVERLAP = 16
 END_GELU = 32
@@ -157,9 +157,12 @@ def tile_picked_edgecv_gelu_e_kernel(
             w1_raw,
             (
                 (nc.vector.tensor_copy, 0, 0, P),
-                (nc.scalar.copy, 1, W1_VECTOR_COLUMNS, P),
                 (nc.vector.tensor_copy, 1, 0, W1_VECTOR_COLUMNS),
             ),
+        )
+        nc.scalar.copy(
+            w1_pairs[1].rearrange("p (t m j) -> p m t j", t=PAIR, j=PACK)[:, W1_VECTOR_COLUMNS:],
+            w1_raw.rearrange("p j (m t) -> p m t j", t=PACK)[:, W1_VECTOR_COLUMNS:, PAIR:, :],
         )
         w1_mx = quantize("w1", w1_woven[:], 2, sbuf("w1_codes", [P, H], U32))
         w2_woven = sbuf("w2_woven", [P, H * PACK], BF16)
@@ -172,8 +175,8 @@ def tile_picked_edgecv_gelu_e_kernel(
             ),
         )
         nc.scalar.copy(
-            w2_woven[:].rearrange("p (t m j) -> p m j t", t=PACK, j=PACK)[:, W2_VECTOR_COLUMNS:],
-            w2_raw.rearrange("p j (m t) -> p m j t", t=PACK)[:, W2_VECTOR_COLUMNS:],
+            w2_woven[:].rearrange("p (t m j) -> p m t j", t=PACK, j=PACK)[:, W2_VECTOR_COLUMNS:],
+            w2_raw.rearrange("p j (m t) -> p m t j", t=PACK)[:, W2_VECTOR_COLUMNS:],
         )
         w2_mx = quantize("w2", w2_woven[:], 2, sbuf("w2_codes", [P, H], U32))
 

@@ -27,8 +27,7 @@ QUADRANT = 32
 SCALAR_PLANES = 2
 SCALAR_FIRST_POINTS = 192
 SCALAR_LAST_POINTS = 64
-W1_VECTOR_COLUMNS = 40
-W2_VECTOR_COLUMNS = 100
+W1_VECTOR_COLUMNS = (60, 80)
 
 OVERLAP = 16
 END_GELU = 32
@@ -51,14 +50,16 @@ def tile_picked_edgecv_gelu_e_kernel(
             nc.sync.dma_start(tile[:], src)
             return tile
 
-        def load_weight(raw, w):
-            nc.sync.dma_start(raw, w.rearrange("(p j) c -> p j c", j=PACK))
+        def load_weight(name, w, lo, hi):
+            raw = sbuf(name, [P, PACK, hi - lo], F32)
+            nc.sync.dma_start(raw[:], w.rearrange("(p j) c -> p j c", j=PACK)[:, :, lo:hi])
+            return raw
 
         w3_bytes = sbuf("w3_bytes", [P, N], U8)
-        nc.vector.memset(w3_bytes[:].bitcast(I32), 0)
+        nc.gpsimd.memset(w3_bytes[:].bitcast(I32), 0)
 
         warm = sbuf("warm", [P, 8], F32)
-        nc.vector.memset(warm[:], 0.0)
+        nc.gpsimd.memset(warm[:], 0.0)
         nc.scalar.activation(warm[:, 4:5], warm[:, 0:1], GELU)
 
         x_rows = xT.rearrange("(p j) t -> p j t", j=PACK)
@@ -67,12 +68,8 @@ def tile_picked_edgecv_gelu_e_kernel(
         offs_sb = load_list("offs_sb", offs)
         for j in range(1, PACK):
             nc.sync.dma_start(x_planes[j][:], x_rows[:, j, :])
-        w1_tile = sbuf("w1_raw", [P, PACK, H], F32)
-        w1_raw = w1_tile[:]
-        load_weight(w1_raw, w1)
-        w2_then_y = sbuf("w2_then_y", [P, PACK * H + S - OVERLAP], F32)
-        w2_raw = w2_then_y[:, : PACK * H].rearrange("p (j c) -> p j c", j=PACK)
-        load_weight(w2_raw, w2)
+        w1_raw = load_weight("w1_raw", w1, 0, H)
+        w2_halves = [load_weight(f"w2_raw{a}", w2, a * H // 2, (a + 1) * H // 2) for a in range(2)]
         cen_sb = load_list("cen_sb", cen)
         pos_sb = [load_list(f"pos_sb{d}", src) for d, src in enumerate((pos1, pos2, pos3))]
         w3_codes = sbuf("w3_codes", [P, N], I32)
@@ -83,12 +80,7 @@ def tile_picked_edgecv_gelu_e_kernel(
                 w3_scales[0, 4 * q : 4 * q + 4, :].bitcast(I32),
             )
 
-        pair_width = PAIR * P * PACK
-        x_woven_tile = sbuf("x_woven", [P, S * PACK], BF16)
-        x_woven = x_woven_tile[:].rearrange("p (s j) -> p s j", j=PACK)
-        w1_woven = sbuf("w1_woven", [P, H * PACK], BF16)
-        w1_pairs = (w1_woven[:, :pair_width], w1_woven[:, pair_width:])
-
+        x_woven = sbuf("x_woven", [P, S, PACK], BF16)
         picked = sbuf("picked", [P, PACK, S], BF16)
         for j in range(SCALAR_PLANES):
             rounded = sbuf(f"x_rounded{j}", [P, T], BF16)
@@ -118,22 +110,23 @@ def tile_picked_edgecv_gelu_e_kernel(
                 picked[:, :, lo:hi].rearrange("p j (c i) -> p c j i", i=RUN),
             )
 
-        def round_weight(pairs, raw, shares):
-            for engine_copy, u, lo, hi in shares:
-                engine_copy(
-                    pairs[u].rearrange("p (t m j) -> p m j t", t=PAIR, j=PACK)[:, lo:hi],
-                    raw.rearrange("p j (m t) -> p m j t", t=PACK)[:, lo:hi, :, PAIR * u : PAIR * (u + 1)],
-                )
+        def round_pair(engine_copy, woven, first, raw, u, lo, hi):
+            tiles = slice(PAIR * u, PAIR * (u + 1))
+            engine_copy(
+                woven[:].rearrange("p (t m j) -> p m j t", t=PACK, j=PACK)[:, first + lo : first + hi, :, tiles],
+                raw[:].rearrange("p j (m t) -> p m j t", t=PACK)[:, lo:hi, :, tiles],
+            )
 
-        def quantize(name, woven, pieces, codes):
-            width = woven.shape[1] // PACK
-            scale_bytes = sbuf(f"{name}_bytes", [P, width], U8)
-            for lo in range(0, width, width // pieces):
-                hi = lo + width // pieces
+        def quantize(name, woven, cuts, codes):
+            scale_bytes = sbuf(f"{name}_bytes", [P, cuts[-1]], U8)
+            for lo, hi in zip(cuts, cuts[1:]):
                 nc.vector.quantize_mx(
                     codes[:, lo:hi].bitcast(FP8X4), scale_bytes[:, lo:hi], woven[:, PACK * lo : PACK * hi]
                 )
             return codes, scale_bytes
+
+        def flat(tile, lo, hi):
+            return tile[:, lo:hi, :].rearrange("p v t -> p (v t)")
 
         def multiply(bank, lhs, lhs_cols, rhs, rhs_cols):
             nc.tensor.matmul_mx(
@@ -146,51 +139,35 @@ def tile_picked_edgecv_gelu_e_kernel(
                 stop=True,
             )
 
-        def hidden_rows(weight, first_col, rows, bank_no):
+        def hidden_rows(name, weight, t, bank_no):
             bank = psum.tile([P, S], F32, name=f"bank{bank_no}", tag=f"bank{bank_no}")
-            multiply(bank[:], weight, slice(first_col, first_col + P), x_mx, slice(0, S))
-            nc.scalar.copy(rows, bank[:])
+            multiply(bank[:], weight, slice(t * P, (t + 1) * P), x_mx, slice(0, S))
+            rows = sbuf(f"{name}_rows{t}", [P, S], F32)
+            nc.scalar.copy(rows[:], bank[:])
+            return rows
 
-        x_mx = quantize("x", x_woven_tile[:], 2, sbuf("x_codes", [P, S], U32))
-        round_weight(
-            w1_pairs,
-            w1_raw,
-            (
-                (nc.vector.tensor_copy, 0, 0, P),
-                (nc.vector.tensor_copy, 1, 0, W1_VECTOR_COLUMNS),
-            ),
-        )
-        nc.scalar.copy(
-            w1_pairs[1].rearrange("p (t m j) -> p m t j", t=PAIR, j=PACK)[:, W1_VECTOR_COLUMNS:],
-            w1_raw.rearrange("p j (m t) -> p m t j", t=PACK)[:, W1_VECTOR_COLUMNS:, PAIR:, :],
-        )
-        w1_mx = quantize("w1", w1_woven[:], 2, sbuf("w1_codes", [P, H], U32))
+        x_mx = quantize("x", flat(x_woven, 0, S), (0, S // 2, S), sbuf("x_codes", [P, S], U32))
+
+        w1_woven = sbuf("w1_woven", [P, H * PACK], BF16)
+        for u in range(PACK // PAIR):
+            round_pair(nc.vector.tensor_copy, w1_woven, 0, w1_raw, u, 0, W1_VECTOR_COLUMNS[u])
+            round_pair(nc.scalar.copy, w1_woven, 0, w1_raw, u, W1_VECTOR_COLUMNS[u], P)
+        w1_mx = quantize("w1", w1_woven[:], (0, P, PAIR * P, H), sbuf("w1_codes", [P, H], U32))
+
         w2_woven = sbuf("w2_woven", [P, H * PACK], BF16)
-        round_weight(
-            (w2_woven[:, :pair_width], w2_woven[:, pair_width:]),
-            w2_raw,
-            (
-                (nc.vector.tensor_copy, 0, 0, W2_VECTOR_COLUMNS),
-                (nc.vector.tensor_copy, 1, 0, W2_VECTOR_COLUMNS),
-            ),
-        )
         nc.scalar.copy(
-            w2_woven[:].rearrange("p (t m j) -> p m t j", t=PACK, j=PACK)[:, W2_VECTOR_COLUMNS:],
-            w2_raw.rearrange("p j (m t) -> p m t j", t=PACK)[:, W2_VECTOR_COLUMNS:],
+            w2_woven[:].rearrange("p (t m j) -> p m t j", t=PACK, j=PACK)[:, : P // 2],
+            w2_halves[0][:].rearrange("p j (m t) -> p m t j", t=PACK),
         )
-        w2_mx = quantize("w2", w2_woven[:], 2, sbuf("w2_codes", [P, H], U32))
+        for u in range(PACK // PAIR):
+            round_pair(nc.vector.tensor_copy, w2_woven, P // 2, w2_halves[1], u, 0, P // 2)
+        w2_mx = quantize("w2", w2_woven[:], (0, PAIR * P, H), sbuf("w2_codes", [P, H], U32))
 
-        y_first = (PACK * H - OVERLAP, 0, S, 2 * S)
-        y_rows = [w2_then_y[:, first : first + S] for first in y_first]
-        e_rows = [sbuf(f"e_rows{t}", [P, S], F32) for t in range(PACK)]
-        for t in range(PACK):
-            hidden_rows(w1_mx, t * P, y_rows[t], t)
-        for t in range(PACK):
-            hidden_rows(w2_mx, t * P, e_rows[t][:], PACK + t)
-
+        y_rows = [hidden_rows("y", w1_mx, t, t) for t in range(PACK)]
+        e_rows = [hidden_rows("e", w2_mx, t, PACK + t) for t in range(PACK)]
         centre = sbuf("centre", [P, PACK, V], F32)
         for t in range(PACK):
-            nc.vector.tensor_copy(centre[:, t, :], y_rows[t].indirect(cen_sb[:]))
+            nc.vector.tensor_copy(centre[:, t, :], y_rows[t][:].indirect(cen_sb[:]))
 
         edges = sbuf("edges", [P, PACK + 1, 3 * V - 2 * OVERLAP], F32)
         edge = (
@@ -215,9 +192,6 @@ def tile_picked_edgecv_gelu_e_kernel(
                 edge[d][:, :, lo:hi].rearrange("p t (c i) -> p c t i", i=RUN),
                 GELU,
             )
-
-        def flat(tile, lo, hi):
-            return tile[:, lo:hi, :].rearrange("p v t -> p (v t)")
 
         halves = ((0, V // 2), (V // 2, V))
         edge_sums(0, 0, V, range(PACK))
@@ -244,7 +218,7 @@ def tile_picked_edgecv_gelu_e_kernel(
             reuse.tile([P, V // 2], U32, name="z0_codes", offset=0, align_bytes=64),
             sbuf("z1_codes", [P, V // 2], U32),
         ]
-        z_mx = [quantize(f"z{g}", flat(z, lo, hi), 1, z_codes[g]) for g, (lo, hi) in enumerate(halves)]
+        z_mx = [quantize(f"z{g}", flat(z, lo, hi), (0, hi - lo), z_codes[g]) for g, (lo, hi) in enumerate(halves)]
 
         ways_out = ((nc.scalar.copy, nc.scalar), (nc.vector.tensor_copy, nc.sync))
         for g, (lo, hi) in enumerate(halves):

@@ -21,6 +21,7 @@ P = 128
 PACK = 4
 PAIR = 2
 RUN = 4
+LINE_RUN = 2
 LIST_ROWS = 16
 QUADRANT = 32
 
@@ -186,10 +187,10 @@ def tile_picked_edgecv_gelu_e_kernel(
                     ADD,
                 )
 
-        def gelu(d, lo, hi):
+        def gelu(d, lo, hi, run=RUN):
             nc.scalar.activation(
-                act[d][:, lo:hi, :].rearrange("p (c i) t -> p c t i", i=RUN),
-                edge[d][:, :, lo:hi].rearrange("p t (c i) -> p c t i", i=RUN),
+                act[d][:, lo:hi, :].rearrange("p (c i) t -> p c t i", i=run),
+                edge[d][:, :, lo:hi].rearrange("p t (c i) -> p c t i", i=run),
                 GELU,
             )
 
@@ -203,7 +204,7 @@ def tile_picked_edgecv_gelu_e_kernel(
         edge_sums(2, 0, V, range(PAIR))
         for lo, hi in halves:
             edge_sums(2, lo, hi, range(PAIR, PACK))
-            gelu(2, lo, hi)
+            gelu(2, lo, hi, LINE_RUN)
 
         best_two = [
             sbuf("best_two0", [P, V // 2 * PACK], BF16),

@@ -24,14 +24,9 @@ RUN = 4
 LINE_RUN = 2
 LIST_ROWS = 16
 QUADRANT = 32
-
-SCALAR_PLANES = 2
-SCALAR_FIRST_POINTS = 192
-SCALAR_LAST_POINTS = 64
-W1_VECTOR_COLUMNS = (60, 80)
-
+VECTOR_WEAVE = 304
 OVERLAP = 16
-END_GELU = 32
+FIRST_GELU = 32
 
 
 def tile_picked_edgecv_gelu_e_kernel(
@@ -41,6 +36,7 @@ def tile_picked_edgecv_gelu_e_kernel(
     with ExitStack() as ctx:
         keep = ctx.enter_context(tc.tile_pool(name="keep", bufs=1))
         reuse = ctx.enter_context(tc.tile_pool(name="reuse", bufs=1))
+        late = ctx.enter_context(tc.tile_pool(name="late", bufs=1))
         psum = ctx.enter_context(tc.psum_pool(name="psum", bufs=1))
 
         def sbuf(name, shape, dtype):
@@ -51,10 +47,13 @@ def tile_picked_edgecv_gelu_e_kernel(
             nc.sync.dma_start(tile[:], src)
             return tile
 
-        def load_weight(name, w, lo, hi):
-            raw = sbuf(name, [P, PACK, hi - lo], F32)
-            nc.sync.dma_start(raw[:], w.rearrange("(p j) c -> p j c", j=PACK)[:, :, lo:hi])
+        def load_half(name, w, a):
+            raw = sbuf(name, [P, PACK, H // 2], F32)
+            nc.sync.dma_start(raw[:], w.rearrange("(p j) c -> p j c", j=PACK)[:, :, a * H // 2 : (a + 1) * H // 2])
             return raw
+
+        def entries(tile, lo, hi):
+            return tile[:, lo // LIST_ROWS : hi // LIST_ROWS]
 
         w3_bytes = sbuf("w3_bytes", [P, N], U8)
         nc.gpsimd.memset(w3_bytes[:].bitcast(I32), 0)
@@ -69,8 +68,8 @@ def tile_picked_edgecv_gelu_e_kernel(
         offs_sb = load_list("offs_sb", offs)
         for j in range(1, PACK):
             nc.sync.dma_start(x_planes[j][:], x_rows[:, j, :])
-        w1_raw = load_weight("w1_raw", w1, 0, H)
-        w2_halves = [load_weight(f"w2_raw{a}", w2, a * H // 2, (a + 1) * H // 2) for a in range(2)]
+        w1_halves = [load_half(f"w1_raw{a}", w1, a) for a in range(2)]
+        w2_halves = [load_half(f"w2_raw{a}", w2, a) for a in range(2)]
         cen_sb = load_list("cen_sb", cen)
         pos_sb = [load_list(f"pos_sb{d}", src) for d, src in enumerate((pos1, pos2, pos3))]
         w3_codes = sbuf("w3_codes", [P, N], I32)
@@ -81,50 +80,38 @@ def tile_picked_edgecv_gelu_e_kernel(
                 w3_scales[0, 4 * q : 4 * q + 4, :].bitcast(I32),
             )
 
+        def scalar_gather(dst, window):
+            nc.scalar.activation(dst, window, COPY)
+
         x_woven = sbuf("x_woven", [P, S, PACK], BF16)
         picked = sbuf("picked", [P, PACK, S], BF16)
-        for j in range(SCALAR_PLANES):
-            rounded = sbuf(f"x_rounded{j}", [P, T], BF16)
-            nc.vector.tensor_copy(rounded[:], x_planes[j][:])
-            nc.scalar.activation(picked[:, j, :], rounded[:].indirect(offs_sb[:]), COPY)
-        for j in range(SCALAR_PLANES, PACK - 1):
-            nc.vector.tensor_copy(picked[:, j, :], x_planes[j][:].indirect(offs_sb[:]))
-        point_shares = (
-            (nc.scalar.copy, 0, SCALAR_FIRST_POINTS),
-            (nc.vector.tensor_copy, SCALAR_FIRST_POINTS, S - SCALAR_LAST_POINTS),
-            (nc.scalar.copy, S - SCALAR_LAST_POINTS, S),
-        )
-        for engine_copy, lo, hi in point_shares:
-            nc.vector.tensor_copy(
-                picked[:, PACK - 1, lo:hi],
-                x_planes[PACK - 1][:].indirect(offs_sb[:, lo // LIST_ROWS : hi // LIST_ROWS]),
-            )
-        weave_shares = (
-            point_shares[0],
-            (nc.vector.tensor_copy, SCALAR_FIRST_POINTS, S // 2),
-            (nc.vector.tensor_copy, S // 2, S - SCALAR_LAST_POINTS),
-            point_shares[2],
-        )
-        for engine_copy, lo, hi in weave_shares:
+        gathers = (scalar_gather, nc.vector.tensor_copy)
+        for j in range(PACK - 1):
+            gathers[j % 2](picked[:, j, :], x_planes[j][:].indirect(offs_sb[:]))
+        for gather, lo, hi in ((nc.vector.tensor_copy, 0, S // 2), (scalar_gather, S // 2, S)):
+            gather(picked[:, PACK - 1, lo:hi], x_planes[PACK - 1][:].indirect(entries(offs_sb, lo, hi)))
+        for engine_copy, lo, hi in (
+            (nc.vector.tensor_copy, 0, S // 2),
+            (nc.vector.tensor_copy, S // 2, VECTOR_WEAVE),
+            (nc.scalar.copy, VECTOR_WEAVE, S),
+        ):
             engine_copy(
                 x_woven[:, lo:hi, :].rearrange("p (c i) j -> p c j i", i=RUN),
                 picked[:, :, lo:hi].rearrange("p j (c i) -> p c j i", i=RUN),
             )
 
-        def round_pair(engine_copy, woven, first, raw, u, lo, hi):
+        def round_pair(engine_copy, woven, halves, a, u):
             tiles = slice(PAIR * u, PAIR * (u + 1))
             engine_copy(
-                woven[:].rearrange("p (t m j) -> p m j t", t=PACK, j=PACK)[:, first + lo : first + hi, :, tiles],
-                raw[:].rearrange("p j (m t) -> p m j t", t=PACK)[:, lo:hi, :, tiles],
+                woven[:].rearrange("p (t m j) -> p m j t", t=PACK, j=PACK)[:, a * P // 2 : (a + 1) * P // 2, :, tiles],
+                halves[a][:].rearrange("p j (m t) -> p m j t", t=PACK)[:, :, :, tiles],
             )
 
-        def quantize(name, woven, cuts, codes):
-            scale_bytes = sbuf(f"{name}_bytes", [P, cuts[-1]], U8)
-            for lo, hi in zip(cuts, cuts[1:]):
-                nc.vector.quantize_mx(
-                    codes[:, lo:hi].bitcast(FP8X4), scale_bytes[:, lo:hi], woven[:, PACK * lo : PACK * hi]
-                )
-            return codes, scale_bytes
+        def operand(name, width):
+            return sbuf(f"{name}_codes", [P, width], U32), sbuf(f"{name}_bytes", [P, width], U8)
+
+        def quantize(mx, woven, lo, hi):
+            nc.vector.quantize_mx(mx[0][:, lo:hi].bitcast(FP8X4), mx[1][:, lo:hi], woven[:, PACK * lo : PACK * hi])
 
         def flat(tile, lo, hi):
             return tile[:, lo:hi, :].rearrange("p v t -> p (v t)")
@@ -140,51 +127,68 @@ def tile_picked_edgecv_gelu_e_kernel(
                 stop=True,
             )
 
-        def hidden_rows(name, weight, t, bank_no):
-            bank = psum.tile([P, S], F32, name=f"bank{bank_no}", tag=f"bank{bank_no}")
-            multiply(bank[:], weight, slice(t * P, (t + 1) * P), x_mx, slice(0, S))
-            rows = sbuf(f"{name}_rows{t}", [P, S], F32)
-            nc.scalar.copy(rows[:], bank[:])
-            return rows
+        def hidden_rows(name, weight, t, banks, engine_copy, rows):
+            width = S // len(banks)
+            for n, bank_no in enumerate(banks):
+                cols = slice(n * width, (n + 1) * width)
+                bank = psum.tile([P, width], F32, name=f"bank_{name}{t}{n}", tag=f"bank{bank_no}")
+                multiply(bank[:], weight, slice(t * P, (t + 1) * P), x_mx, cols)
+                engine_copy(rows[:, cols], bank[:])
 
-        x_mx = quantize("x", flat(x_woven, 0, S), (0, S // 2, S), sbuf("x_codes", [P, S], U32))
+        x_mx = operand("x", S)
+        quantize(x_mx, flat(x_woven, 0, S), 0, S // 2)
+        quantize(x_mx, flat(x_woven, 0, S), S // 2, S)
 
         w1_woven = sbuf("w1_woven", [P, H * PACK], BF16)
+        w2_woven = late.tile([P, H * PACK], BF16, name="w2_woven", offset=0, align_bytes=64)
+        w1_mx = operand("w1", H)
+        w2_mx = operand("w2", H)
+        round_pair(nc.scalar.copy, w1_woven, w1_halves, 0, 0)
+        round_pair(nc.vector.tensor_copy, w1_woven, w1_halves, 1, 0)
+        quantize(w1_mx, w1_woven[:], 0, P)
+        quantize(w1_mx, w1_woven[:], P, PAIR * P)
+        round_pair(nc.scalar.copy, w1_woven, w1_halves, 0, 1)
+        round_pair(nc.scalar.copy, w1_woven, w1_halves, 1, 1)
+        round_pair(nc.scalar.copy, w2_woven, w2_halves, 0, 0)
+        round_pair(nc.vector.tensor_copy, w2_woven, w2_halves, 0, 1)
+        quantize(w1_mx, w1_woven[:], PAIR * P, H)
         for u in range(PACK // PAIR):
-            round_pair(nc.vector.tensor_copy, w1_woven, 0, w1_raw, u, 0, W1_VECTOR_COLUMNS[u])
-            round_pair(nc.scalar.copy, w1_woven, 0, w1_raw, u, W1_VECTOR_COLUMNS[u], P)
-        w1_mx = quantize("w1", w1_woven[:], (0, P, PAIR * P, H), sbuf("w1_codes", [P, H], U32))
+            round_pair(nc.vector.tensor_copy, w2_woven, w2_halves, 1, u)
+        quantize(w2_mx, w2_woven[:], 0, P)
+        quantize(w2_mx, w2_woven[:], P, PAIR * P)
+        quantize(w2_mx, w2_woven[:], PAIR * P, H)
 
-        w2_woven = sbuf("w2_woven", [P, H * PACK], BF16)
-        nc.scalar.copy(
-            w2_woven[:].rearrange("p (t m j) -> p m t j", t=PACK, j=PACK)[:, : P // 2],
-            w2_halves[0][:].rearrange("p j (m t) -> p m t j", t=PACK),
-        )
-        for u in range(PACK // PAIR):
-            round_pair(nc.vector.tensor_copy, w2_woven, P // 2, w2_halves[1], u, 0, P // 2)
-        w2_mx = quantize("w2", w2_woven[:], (0, PAIR * P, H), sbuf("w2_codes", [P, H], U32))
-
-        y_rows = [hidden_rows("y", w1_mx, t, t) for t in range(PACK)]
-        e_rows = [hidden_rows("e", w2_mx, t, PACK + t) for t in range(PACK)]
         centre = sbuf("centre", [P, PACK, V], F32)
-        for t in range(PACK):
-            nc.vector.tensor_copy(centre[:, t, :], y_rows[t][:].indirect(cen_sb[:]))
 
-        edges = sbuf("edges", [P, PACK + 1, 3 * V - 2 * OVERLAP], F32)
-        edge = (
-            edges[:, :PACK, V - OVERLAP : 2 * V - OVERLAP],
-            edges[:, 1:, 2 * (V - OVERLAP) :],
-            edges[:, :PACK, :V],
-        )
+        def centres(t, rows):
+            scalar_gather(centre[:, t, :], rows[:].indirect(cen_sb[:]))
+
+        y_rows = [sbuf(f"y_rows{t}", [P, S], F32) for t in range(PAIR)]
+        for t in range(PAIR, PACK):
+            y_rows.append(late.tile([P, S], F32, name=f"y_rows{t}", offset=(t - PAIR) * S * 4, align_bytes=64))
+        e_rows = [sbuf(f"e_rows{t}", [P, S], F32) for t in range(PACK)]
+        hidden_rows("y", w1_mx, 0, (0, 1), nc.scalar.copy, y_rows[0])
+        hidden_rows("y", w1_mx, 1, (2,), nc.scalar.copy, y_rows[1])
+        centres(0, y_rows[0])
+        centres(1, y_rows[1])
+        hidden_rows("e", w2_mx, 0, (5, 6), nc.vector.tensor_copy, e_rows[0])
+        hidden_rows("e", w2_mx, 1, (7,), nc.scalar.copy, e_rows[1])
+        for t in range(PAIR, PACK):
+            hidden_rows("y", w1_mx, t, (t + 1,), nc.scalar.copy, y_rows[t])
+            hidden_rows("e", w2_mx, t, (t - PAIR,), nc.scalar.copy, e_rows[t])
+            centres(t, y_rows[t])
+        fetched = late.tile([P, V], F32, name="fetched", offset=S * 4, align_bytes=64)
+        scalar_gather(fetched[:], e_rows[0][:].indirect(pos_sb[2][:]))
+
+        edges = sbuf("edges", [P, PACK + 1, 2 * V - OVERLAP], F32)
+        edge1 = sbuf("edge1", [P, PACK, V], F32)
+        edge = (edges[:, 1:, V - OVERLAP :], edge1[:], edges[:, :PACK, :V])
         act = [sbuf(f"act{d}", [P, V, PACK], BF16) for d in range(3)]
 
         def edge_sums(d, lo, hi, tiles):
             for t in tiles:
                 nc.vector.tensor_tensor(
-                    edge[d][:, t, lo:hi],
-                    e_rows[t][:].indirect(pos_sb[d][:, lo // LIST_ROWS : hi // LIST_ROWS]),
-                    centre[:, t, lo:hi],
-                    ADD,
+                    edge[d][:, t, lo:hi], e_rows[t][:].indirect(entries(pos_sb[d], lo, hi)), centre[:, t, lo:hi], ADD
                 )
 
         def gelu(d, lo, hi, run=RUN):
@@ -195,13 +199,14 @@ def tile_picked_edgecv_gelu_e_kernel(
             )
 
         halves = ((0, V // 2), (V // 2, V))
-        edge_sums(0, 0, V, range(PACK))
-        edge_sums(1, 0, V, (PACK - 1,))
-        gelu(0, V - END_GELU, V)
-        edge_sums(1, 0, V, range(PACK - 1))
-        gelu(0, 0, V - END_GELU)
+        for t in range(PACK):
+            edge_sums(0, 0, V, (t,))
+            edge_sums(1, 0, V, (t,))
+        gelu(0, 0, FIRST_GELU)
+        gelu(0, FIRST_GELU, V)
         gelu(1, 0, V)
-        edge_sums(2, 0, V, range(PAIR))
+        nc.vector.tensor_tensor(edge[2][:, 0, :], fetched[:], centre[:, 0, :], ADD)
+        edge_sums(2, 0, V, (1,))
         for lo, hi in halves:
             edge_sums(2, lo, hi, range(PAIR, PACK))
             gelu(2, lo, hi, LINE_RUN)
@@ -215,16 +220,18 @@ def tile_picked_edgecv_gelu_e_kernel(
             nc.vector.tensor_tensor(best_two[g][:], flat(act[0], lo, hi), flat(act[1], lo, hi), MAX)
         for g, (lo, hi) in enumerate(halves):
             nc.vector.tensor_tensor(flat(z, lo, hi), best_two[g][:], flat(act[2], lo, hi), MAX)
-        z_codes = [
-            reuse.tile([P, V // 2], U32, name="z0_codes", offset=0, align_bytes=64),
-            sbuf("z1_codes", [P, V // 2], U32),
+        z_mx = [
+            (reuse.tile([P, V // 2], U32, name="z0_codes", offset=0, align_bytes=64), sbuf("z0_bytes", [P, V // 2], U8)),
+            (sbuf("z1_codes", [P, V // 2], U32), sbuf("z1_bytes", [P, V // 2], U8)),
         ]
-        z_mx = [quantize(f"z{g}", flat(z, lo, hi), (0, hi - lo), z_codes[g]) for g, (lo, hi) in enumerate(halves)]
+        for g, (lo, hi) in enumerate(halves):
+            quantize(z_mx[g], flat(z, lo, hi), 0, hi - lo)
 
         ways_out = ((nc.scalar.copy, nc.scalar), (nc.vector.tensor_copy, nc.sync))
+        out_banks = (2, 3, 4, 5)
         for g, (lo, hi) in enumerate(halves):
             for h, (engine_copy, queue) in enumerate(ways_out):
-                bank = psum.tile([P, hi - lo], F32, name=f"out_bank{g}{h}", tag=f"bank{1 + len(ways_out) * g + h}")
+                bank = psum.tile([P, hi - lo], F32, name=f"out_bank{g}{h}", tag=f"bank{out_banks[2 * g + h]}")
                 multiply(bank[:], (w3_codes, w3_bytes), slice(h * P, (h + 1) * P), z_mx[g], slice(0, hi - lo))
                 staged = sbuf(f"staged{g}{h}", [P, hi - lo], F32)
                 engine_copy(staged[:], bank[:])

@@ -172,7 +172,7 @@ def tile_picked_edgecv_gelu_e_kernel(
         centres(0, y_rows[0])
         centres(1, y_rows[1])
         hidden_rows("e", w2_mx, 0, (5, 6), nc.vector.tensor_copy, e_rows[0])
-        hidden_rows("e", w2_mx, 1, (7,), nc.scalar.copy, e_rows[1])
+        hidden_rows("e", w2_mx, 1, (7,), nc.vector.tensor_copy, e_rows[1])
         for t in range(PAIR, PACK):
             hidden_rows("y", w1_mx, t, (t + 1,), nc.scalar.copy, y_rows[t])
             hidden_rows("e", w2_mx, t, (t - PAIR,), nc.scalar.copy, e_rows[t])

@@ -24,9 +24,11 @@ RUN = 4
 LINE_RUN = 2
 LIST_ROWS = 16
 QUADRANT = 32
-VECTOR_WEAVE = 304
-OVERLAP = 16
-FIRST_GELU = 32
+VECTOR_WEAVE = 320
+FETCHED = 2
+W1_VECTOR_COLUMNS = 92
+W2_CUT = 80
+W2_VECTOR_COLUMNS = 60
 
 
 def tile_picked_edgecv_gelu_e_kernel(
@@ -47,9 +49,9 @@ def tile_picked_edgecv_gelu_e_kernel(
             nc.sync.dma_start(tile[:], src)
             return tile
 
-        def load_half(name, w, a):
-            raw = sbuf(name, [P, PACK, H // 2], F32)
-            nc.sync.dma_start(raw[:], w.rearrange("(p j) c -> p j c", j=PACK)[:, :, a * H // 2 : (a + 1) * H // 2])
+        def load_weight(name, w, lo, hi):
+            raw = sbuf(name, [P, PACK, hi - lo], F32)
+            nc.sync.dma_start(raw[:], w.rearrange("(p j) c -> p j c", j=PACK)[:, :, lo:hi])
             return raw
 
         def entries(tile, lo, hi):
@@ -68,8 +70,8 @@ def tile_picked_edgecv_gelu_e_kernel(
         offs_sb = load_list("offs_sb", offs)
         for j in range(1, PACK):
             nc.sync.dma_start(x_planes[j][:], x_rows[:, j, :])
-        w1_halves = [load_half(f"w1_raw{a}", w1, a) for a in range(2)]
-        w2_halves = [load_half(f"w2_raw{a}", w2, a) for a in range(2)]
+        w1_raw = load_weight("w1_raw", w1, 0, H)
+        w2_halves = [load_weight("w2_raw0", w2, 0, PACK * W2_CUT), load_weight("w2_raw1", w2, PACK * W2_CUT, H)]
         cen_sb = load_list("cen_sb", cen)
         pos_sb = [load_list(f"pos_sb{d}", src) for d, src in enumerate((pos1, pos2, pos3))]
         w3_codes = sbuf("w3_codes", [P, N], I32)
@@ -100,11 +102,11 @@ def tile_picked_edgecv_gelu_e_kernel(
                 picked[:, :, lo:hi].rearrange("p j (c i) -> p c j i", i=RUN),
             )
 
-        def round_pair(engine_copy, woven, halves, a, u):
+        def round_pair(engine_copy, woven, first, raw, u, lo, hi):
             tiles = slice(PAIR * u, PAIR * (u + 1))
             engine_copy(
-                woven[:].rearrange("p (t m j) -> p m j t", t=PACK, j=PACK)[:, a * P // 2 : (a + 1) * P // 2, :, tiles],
-                halves[a][:].rearrange("p j (m t) -> p m j t", t=PACK)[:, :, :, tiles],
+                woven[:].rearrange("p (t m j) -> p m j t", t=PACK, j=PACK)[:, first + lo : first + hi, :, tiles],
+                raw[:].rearrange("p j (m t) -> p m j t", t=PACK)[:, lo:hi, :, tiles],
             )
 
         def operand(name, width):
@@ -127,9 +129,9 @@ def tile_picked_edgecv_gelu_e_kernel(
                 stop=True,
             )
 
-        def hidden_rows(name, weight, t, banks, engine_copy, rows):
-            width = S // len(banks)
-            for n, bank_no in enumerate(banks):
+        def hidden_rows(name, weight, t, ways, rows):
+            width = S // len(ways)
+            for n, (bank_no, engine_copy) in enumerate(ways):
                 cols = slice(n * width, (n + 1) * width)
                 bank = psum.tile([P, width], F32, name=f"bank_{name}{t}{n}", tag=f"bank{bank_no}")
                 multiply(bank[:], weight, slice(t * P, (t + 1) * P), x_mx, cols)
@@ -137,52 +139,54 @@ def tile_picked_edgecv_gelu_e_kernel(
 
         x_mx = operand("x", S)
         quantize(x_mx, flat(x_woven, 0, S), 0, S // 2)
-        quantize(x_mx, flat(x_woven, 0, S), S // 2, S)
 
         w1_woven = sbuf("w1_woven", [P, H * PACK], BF16)
         w2_woven = late.tile([P, H * PACK], BF16, name="w2_woven", offset=0, align_bytes=64)
         w1_mx = operand("w1", H)
         w2_mx = operand("w2", H)
-        round_pair(nc.scalar.copy, w1_woven, w1_halves, 0, 0)
-        round_pair(nc.vector.tensor_copy, w1_woven, w1_halves, 1, 0)
+        round_pair(nc.vector.tensor_copy, w1_woven, 0, w1_raw, 0, 0, W1_VECTOR_COLUMNS)
+        round_pair(nc.scalar.copy, w1_woven, 0, w1_raw, 0, W1_VECTOR_COLUMNS, P)
+        quantize(x_mx, flat(x_woven, 0, S), S // 2, 3 * S // 4)
         quantize(w1_mx, w1_woven[:], 0, P)
+        quantize(x_mx, flat(x_woven, 0, S), 3 * S // 4, S)
         quantize(w1_mx, w1_woven[:], P, PAIR * P)
-        round_pair(nc.scalar.copy, w1_woven, w1_halves, 0, 1)
-        round_pair(nc.scalar.copy, w1_woven, w1_halves, 1, 1)
-        round_pair(nc.scalar.copy, w2_woven, w2_halves, 0, 0)
-        round_pair(nc.vector.tensor_copy, w2_woven, w2_halves, 0, 1)
+        round_pair(nc.scalar.copy, w1_woven, 0, w1_raw, 1, 0, P)
+        round_pair(nc.scalar.copy, w2_woven, 0, w2_halves[0], 0, W2_VECTOR_COLUMNS, W2_CUT)
+        round_pair(nc.vector.tensor_copy, w2_woven, 0, w2_halves[0], 0, 0, W2_VECTOR_COLUMNS)
+        round_pair(nc.vector.tensor_copy, w2_woven, 0, w2_halves[0], 1, 0, W2_CUT)
         quantize(w1_mx, w1_woven[:], PAIR * P, H)
         for u in range(PACK // PAIR):
-            round_pair(nc.vector.tensor_copy, w2_woven, w2_halves, 1, u)
+            round_pair(nc.vector.tensor_copy, w2_woven, W2_CUT, w2_halves[1], u, 0, P - W2_CUT)
         quantize(w2_mx, w2_woven[:], 0, P)
-        quantize(w2_mx, w2_woven[:], P, PAIR * P)
-        quantize(w2_mx, w2_woven[:], PAIR * P, H)
+        quantize(w2_mx, w2_woven[:], P, H)
 
         centre = sbuf("centre", [P, PACK, V], F32)
 
         def centres(t, rows):
-            scalar_gather(centre[:, t, :], rows[:].indirect(cen_sb[:]))
+            scalar_gather(centre[:, t, :], rows.indirect(cen_sb[:]))
 
         y_rows = [sbuf(f"y_rows{t}", [P, S], F32) for t in range(PAIR)]
-        for t in range(PAIR, PACK):
-            y_rows.append(late.tile([P, S], F32, name=f"y_rows{t}", offset=(t - PAIR) * S * 4, align_bytes=64))
+        y_rows.append(late.tile([P, S], F32, name="y_rows2", offset=0, align_bytes=64))
+        later_edges = late.tile([P, PACK, 2 * V], F32, name="later_edges", offset=S * 4, align_bytes=64)
+        y_rows = [rows[:] for rows in y_rows] + [later_edges[:, PAIR, :]]
         e_rows = [sbuf(f"e_rows{t}", [P, S], F32) for t in range(PACK)]
-        hidden_rows("y", w1_mx, 0, (0, 1), nc.scalar.copy, y_rows[0])
-        hidden_rows("y", w1_mx, 1, (2,), nc.scalar.copy, y_rows[1])
+        on_scalar, on_vector = nc.scalar.copy, nc.vector.tensor_copy
+        hidden_rows("y", w1_mx, 0, ((0, on_scalar), (1, on_scalar)), y_rows[0])
+        hidden_rows("y", w1_mx, 1, ((2, on_scalar),), y_rows[1])
         centres(0, y_rows[0])
         centres(1, y_rows[1])
-        hidden_rows("e", w2_mx, 0, (5, 6), nc.vector.tensor_copy, e_rows[0])
-        hidden_rows("e", w2_mx, 1, (7,), nc.vector.tensor_copy, e_rows[1])
-        for t in range(PAIR, PACK):
-            hidden_rows("y", w1_mx, t, (t + 1,), nc.scalar.copy, y_rows[t])
-            hidden_rows("e", w2_mx, t, (t - PAIR,), nc.scalar.copy, e_rows[t])
-            centres(t, y_rows[t])
-        fetched = late.tile([P, V], F32, name="fetched", offset=S * 4, align_bytes=64)
-        scalar_gather(fetched[:], e_rows[0][:].indirect(pos_sb[2][:]))
+        hidden_rows("e", w2_mx, 0, ((5, on_vector), (6, on_vector)), e_rows[0])
+        hidden_rows("e", w2_mx, 1, ((7, on_vector),), e_rows[1])
+        hidden_rows("y", w1_mx, 2, ((3, on_scalar),), y_rows[2])
+        hidden_rows("e", w2_mx, 2, ((4, on_vector), (0, on_scalar)), e_rows[2])
+        centres(2, y_rows[2])
+        hidden_rows("y", w1_mx, 3, ((5, on_scalar),), y_rows[3])
+        hidden_rows("e", w2_mx, 3, ((1, on_scalar),), e_rows[3])
+        centres(3, y_rows[3])
+        edge = (sbuf("edge0", [P, PACK, V], F32), later_edges[:, :, :V], later_edges[:, :, V:])
+        for t in range(FETCHED):
+            scalar_gather(edge[2][:, t, :], e_rows[t][:].indirect(pos_sb[2][:]))
 
-        edges = sbuf("edges", [P, PACK + 1, 2 * V - OVERLAP], F32)
-        edge1 = sbuf("edge1", [P, PACK, V], F32)
-        edge = (edges[:, 1:, V - OVERLAP :], edge1[:], edges[:, :PACK, :V])
         act = [sbuf(f"act{d}", [P, V, PACK], BF16) for d in range(3)]
 
         def edge_sums(d, lo, hi, tiles):
@@ -199,16 +203,14 @@ def tile_picked_edgecv_gelu_e_kernel(
             )
 
         halves = ((0, V // 2), (V // 2, V))
-        for t in range(PACK):
-            edge_sums(0, 0, V, (t,))
-            edge_sums(1, 0, V, (t,))
-        gelu(0, 0, FIRST_GELU)
-        gelu(0, FIRST_GELU, V)
+        for tiles in (range(PAIR), range(PAIR, PACK)):
+            edge_sums(0, 0, V, tiles)
+            edge_sums(1, 0, V, tiles)
+        gelu(0, 0, V)
         gelu(1, 0, V)
-        nc.vector.tensor_tensor(edge[2][:, 0, :], fetched[:], centre[:, 0, :], ADD)
-        edge_sums(2, 0, V, (1,))
+        nc.vector.tensor_tensor(edge[2][:, :FETCHED, :], edge[2][:, :FETCHED, :], centre[:, :FETCHED, :], ADD)
         for lo, hi in halves:
-            edge_sums(2, lo, hi, range(PAIR, PACK))
+            edge_sums(2, lo, hi, range(FETCHED, PACK))
             gelu(2, lo, hi, LINE_RUN)
 
         best_two = [
@@ -227,8 +229,8 @@ def tile_picked_edgecv_gelu_e_kernel(
         for g, (lo, hi) in enumerate(halves):
             quantize(z_mx[g], flat(z, lo, hi), 0, hi - lo)
 
-        ways_out = ((nc.scalar.copy, nc.scalar), (nc.vector.tensor_copy, nc.sync))
-        out_banks = (2, 3, 4, 5)
+        ways_out = ((nc.vector.tensor_copy, nc.sync), (nc.scalar.copy, nc.scalar))
+        out_banks = (2, 3, 4, 6)
         for g, (lo, hi) in enumerate(halves):
             for h, (engine_copy, queue) in enumerate(ways_out):
                 bank = psum.tile([P, hi - lo], F32, name=f"out_bank{g}{h}", tag=f"bank{out_banks[2 * g + h]}")

@@ -26,9 +26,9 @@ LIST_ROWS = 16
 QUADRANT = 32
 VECTOR_WEAVE = 320
 FETCHED = 2
-W1_VECTOR_COLUMNS = 92
+W1_VECTOR_COLUMNS = 84
 W2_CUT = 80
-W2_VECTOR_COLUMNS = 60
+W2_VECTOR_COLUMNS = 44
 
 
 def tile_picked_edgecv_gelu_e_kernel(
@@ -178,7 +178,7 @@ def tile_picked_edgecv_gelu_e_kernel(
         hidden_rows("e", w2_mx, 0, ((5, on_vector), (6, on_vector)), e_rows[0])
         hidden_rows("e", w2_mx, 1, ((7, on_vector),), e_rows[1])
         hidden_rows("y", w1_mx, 2, ((3, on_scalar),), y_rows[2])
-        hidden_rows("e", w2_mx, 2, ((4, on_vector), (0, on_scalar)), e_rows[2])
+        hidden_rows("e", w2_mx, 2, ((0, on_scalar),), e_rows[2])
         centres(2, y_rows[2])
         hidden_rows("y", w1_mx, 3, ((5, on_scalar),), y_rows[3])
         hidden_rows("e", w2_mx, 3, ((1, on_scalar),), e_rows[3])

@@ -37,7 +37,6 @@ def tile_picked_edgecv_gelu_e_kernel(
     nc = tc.nc
     with ExitStack() as ctx:
         keep = ctx.enter_context(tc.tile_pool(name="keep", bufs=1))
-        reuse = ctx.enter_context(tc.tile_pool(name="reuse", bufs=1))
         late = ctx.enter_context(tc.tile_pool(name="late", bufs=1))
         psum = ctx.enter_context(tc.psum_pool(name="psum", bufs=1))
 
@@ -65,10 +64,11 @@ def tile_picked_edgecv_gelu_e_kernel(
         nc.scalar.activation(warm[:, 4:5], warm[:, 0:1], GELU)
 
         x_rows = xT.rearrange("(p j) t -> p j t", j=PACK)
-        x_planes = [sbuf(f"x_plane{j}", [P, T], F32) for j in range(PACK)]
-        nc.sync.dma_start(x_planes[0][:], x_rows[:, 0, :])
+        x_first = sbuf("x_first", [P, PAIR * T], F32)
+        nc.sync.dma_start(x_first[:], x_rows[:, :PAIR, :].rearrange("p j t -> p (j t)"))
         offs_sb = load_list("offs_sb", offs)
-        for j in range(1, PACK):
+        x_planes = {j: sbuf(f"x_plane{j}", [P, T], F32) for j in range(PAIR, PACK)}
+        for j in range(PAIR, PACK):
             nc.sync.dma_start(x_planes[j][:], x_rows[:, j, :])
         w1_raw = load_weight("w1_raw", w1, 0, H)
         w2_halves = [load_weight("w2_raw0", w2, 0, PACK * W2_CUT), load_weight("w2_raw1", w2, PACK * W2_CUT, H)]
@@ -86,12 +86,14 @@ def tile_picked_edgecv_gelu_e_kernel(
             nc.scalar.activation(dst, window, COPY)
 
         x_woven = sbuf("x_woven", [P, S, PACK], BF16)
-        picked = sbuf("picked", [P, PACK, S], BF16)
-        gathers = (scalar_gather, nc.vector.tensor_copy)
-        for j in range(PACK - 1):
-            gathers[j % 2](picked[:, j, :], x_planes[j][:].indirect(offs_sb[:]))
-        for gather, lo, hi in ((nc.vector.tensor_copy, 0, S // 2), (scalar_gather, S // 2, S)):
-            gather(picked[:, PACK - 1, lo:hi], x_planes[PACK - 1][:].indirect(entries(offs_sb, lo, hi)))
+        half = S // 2
+        picked = sbuf("picked", [P, 2, PACK, half], BF16)
+        for g in range(2):
+            scalar_gather(picked[:, g, 0, :], x_first[:].indirect(entries(offs_sb, g * half, (g + 1) * half)))
+        nc.vector.tensor_copy(picked[:, :, 1, :], x_first[:, T:].indirect(offs_sb[:]))
+        for j in range(PAIR, PACK):
+            for g, gather in enumerate((nc.vector.tensor_copy, scalar_gather)):
+                gather(picked[:, g, j, :], x_planes[j][:].indirect(entries(offs_sb, g * half, (g + 1) * half)))
         for engine_copy, lo, hi in (
             (nc.vector.tensor_copy, 0, S // 2),
             (nc.vector.tensor_copy, S // 2, VECTOR_WEAVE),
@@ -99,7 +101,7 @@ def tile_picked_edgecv_gelu_e_kernel(
         ):
             engine_copy(
                 x_woven[:, lo:hi, :].rearrange("p (c i) j -> p c j i", i=RUN),
-                picked[:, :, lo:hi].rearrange("p j (c i) -> p c j i", i=RUN),
+                picked[:, lo // half, :, lo % half : (hi - 1) % half + 1].rearrange("p j (c i) -> p c j i", i=RUN),
             )
 
         def round_pair(engine_copy, woven, first, raw, u, lo, hi):
@@ -213,17 +215,14 @@ def tile_picked_edgecv_gelu_e_kernel(
             edge_sums(2, lo, hi, range(FETCHED, PACK))
             gelu(2, lo, hi, LINE_RUN)
 
-        best_two = [
-            sbuf("best_two0", [P, V // 2 * PACK], BF16),
-            reuse.tile([P, V // 2 * PACK], BF16, name="best_two1", offset=0, align_bytes=64),
-        ]
+        best_two = [sbuf(f"best_two{g}", [P, V // 2 * PACK], BF16) for g in range(2)]
         z = sbuf("z", [P, V, PACK], BF16)
         for g, (lo, hi) in enumerate(halves):
             nc.vector.tensor_tensor(best_two[g][:], flat(act[0], lo, hi), flat(act[1], lo, hi), MAX)
         for g, (lo, hi) in enumerate(halves):
             nc.vector.tensor_tensor(flat(z, lo, hi), best_two[g][:], flat(act[2], lo, hi), MAX)
         z_mx = [
-            (reuse.tile([P, V // 2], U32, name="z0_codes", offset=0, align_bytes=64), sbuf("z0_bytes", [P, V // 2], U8)),
+            (late.tile([P, V // 2], U32, name="z0_codes", offset=S * 4, align_bytes=64), sbuf("z0_bytes", [P, V // 2], U8)),
             (sbuf("z1_codes", [P, V // 2], U32), sbuf("z1_bytes", [P, V // 2], U8)),
         ]
         for g, (lo, hi) in enumerate(halves):

@@ -178,7 +178,7 @@ def tile_picked_edgecv_gelu_e_kernel(
         centres(0, y_rows[0])
         centres(1, y_rows[1])
         hidden_rows("e", w2_mx, 0, ((5, on_vector), (6, on_vector)), e_rows[0])
-        hidden_rows("e", w2_mx, 1, ((7, on_vector),), e_rows[1])
+        hidden_rows("e", w2_mx, 1, ((7, on_vector), (4, on_scalar)), e_rows[1])
         hidden_rows("y", w1_mx, 2, ((3, on_scalar),), y_rows[2])
         hidden_rows("e", w2_mx, 2, ((0, on_scalar),), e_rows[2])
         centres(2, y_rows[2])

from contextlib import ExitStack

import concourse.mybir as mybir

K, T, S, V, H, N = 512, 1024, 512, 256, 512, 256
FLOPS = 2 * 2 * K * H * S + 2 * H * N * V

F32 = mybir.dt.float32
BF16 = mybir.dt.bfloat16
I32 = mybir.dt.int32
U32 = mybir.dt.uint32
U16 = mybir.dt.uint16
U8 = mybir.dt.uint8
FP8X4 = mybir.dt.float8_e4m3fn_x4
ADD = mybir.AluOpType.add
MAX = mybir.AluOpType.max
COPY = mybir.ActivationFunctionType.Copy
GELU = mybir.ActivationFunctionType.Gelu_apprx_tanh

P = 128
PACK = 4
PAIR = 2
RUN = 4
LINE_RUN = 2
LIST_ROWS = 16
QUADRANT = 32
VECTOR_WEAVE = 320
FETCHED = 2
W1_VECTOR_COLUMNS = 84
W2_CUT = 80
W2_VECTOR_COLUMNS = 44


def tile_picked_edgecv_gelu_e_kernel(
    tc, xT, w1, w2, w3_words, w3_scales, offs, cen, pos1, pos2, pos3, out
):
    nc = tc.nc
    with ExitStack() as ctx:
        keep = ctx.enter_context(tc.tile_pool(name="keep", bufs=1))
        late = ctx.enter_context(tc.tile_pool(name="late", bufs=1))
        psum = ctx.enter_context(tc.psum_pool(name="psum", bufs=1))

        def sbuf(name, shape, dtype):
            return keep.tile(shape, dtype, name=name, tag=name, align_bytes=64)

        def load_list(name, src):
            tile = keep.tile(list(src.shape), U16, name=name)
            nc.sync.dma_start(tile[:], src)
            return tile

        def load_weight(name, w, lo, hi):
            raw = sbuf(name, [P, PACK, hi - lo], F32)
            nc.sync.dma_start(raw[:], w.rearrange("(p j) c -> p j c", j=PACK)[:, :, lo:hi])
            return raw

        def entries(tile, lo, hi):
            return tile[:, lo // LIST_ROWS : hi // LIST_ROWS]

        w3_bytes = sbuf("w3_bytes", [P, N], U8)
        nc.gpsimd.memset(w3_bytes[:].bitcast(I32), 0)

        warm = sbuf("warm", [P, 8], F32)
        nc.gpsimd.memset(warm[:], 0.0)
        nc.scalar.activation(warm[:, 4:5], warm[:, 0:1], GELU)

        x_rows = xT.rearrange("(p j) t -> p j t", j=PACK)
        x_first = sbuf("x_first", [P, PAIR * T], F32)
        nc.sync.dma_start(x_first[:], x_rows[:, :PAIR, :].rearrange("p j t -> p (j t)"))
        offs_sb = load_list("offs_sb", offs)
        x_planes = {j: sbuf(f"x_plane{j}", [P, T], F32) for j in range(PAIR, PACK)}
        for j in range(PAIR, PACK):
            nc.sync.dma_start(x_planes[j][:], x_rows[:, j, :])
        w1_raw = load_weight("w1_raw", w1, 0, H)
        w2_halves = [load_weight("w2_raw0", w2, 0, PACK * W2_CUT), load_weight("w2_raw1", w2, PACK * W2_CUT, H)]
        cen_sb = load_list("cen_sb", cen)
        pos_sb = [load_list(f"pos_sb{d}", src) for d, src in enumerate((pos1, pos2, pos3))]
        w3_codes = sbuf("w3_codes", [P, N], I32)
        nc.sync.dma_start(w3_codes[:], w3_words[0].rearrange("p n t -> p (n t)").bitcast(I32))
        for q in range(P // QUADRANT):
            nc.sync.dma_start(
                w3_bytes[QUADRANT * q : QUADRANT * q + 4, :].bitcast(I32),
                w3_scales[0, 4 * q : 4 * q + 4, :].bitcast(I32),
            )

        def scalar_gather(dst, window):
            nc.scalar.activation(dst, window, COPY)

        x_woven = sbuf("x_woven", [P, S, PACK], BF16)
        half = S // 2
        picked = sbuf("picked", [P, 2, PACK, half], BF16)
        for g in range(2):
            scalar_gather(picked[:, g, 0, :], x_first[:].indirect(entries(offs_sb, g * half, (g + 1) * half)))
        nc.vector.tensor_copy(picked[:, :, 1, :], x_first[:, T:].indirect(offs_sb[:]))
        for j in range(PAIR, PACK):
            for g, gather in enumerate((nc.vector.tensor_copy, scalar_gather)):
                gather(picked[:, g, j, :], x_planes[j][:].indirect(entries(offs_sb, g * half, (g + 1) * half)))
        for engine_copy, lo, hi in (
            (nc.vector.tensor_copy, 0, S // 2),
            (nc.vector.tensor_copy, S // 2, VECTOR_WEAVE),
            (nc.scalar.copy, VECTOR_WEAVE, S),
        ):
            engine_copy(
                x_woven[:, lo:hi, :].rearrange("p (c i) j -> p c j i", i=RUN),
                picked[:, lo // half, :, lo % half : (hi - 1) % half + 1].rearrange("p j (c i) -> p c j i", i=RUN),
            )

        def round_pair(engine_copy, woven, first, raw, u, lo, hi):
            tiles = slice(PAIR * u, PAIR * (u + 1))
            engine_copy(
                woven[:].rearrange("p (t m j) -> p m j t", t=PACK, j=PACK)[:, first + lo : first + hi, :, tiles],
                raw[:].rearrange("p j (m t) -> p m j t", t=PACK)[:, lo:hi, :, tiles],
            )

        def operand(name, width):
            return sbuf(f"{name}_codes", [P, width], U32), sbuf(f"{name}_bytes", [P, width], U8)

        def quantize(mx, woven, lo, hi):
            nc.vector.quantize_mx(mx[0][:, lo:hi].bitcast(FP8X4), mx[1][:, lo:hi], woven[:, PACK * lo : PACK * hi])

        def flat(tile, lo, hi):
            return tile[:, lo:hi, :].rearrange("p v t -> p (v t)")

        def multiply(bank, lhs, lhs_cols, rhs, rhs_cols):
            nc.tensor.matmul_mx(
                bank,
                lhsT=lhs[0][:, lhs_cols].bitcast(FP8X4),
                lhsT_scale=lhs[1][:, lhs_cols],
                rhs=rhs[0][:, rhs_cols].bitcast(FP8X4),
                rhs_scale=rhs[1][:, rhs_cols],
                start=True,
                stop=True,
            )

        def hidden_rows(name, weight, t, ways, rows):
            width = S // len(ways)
            for n, (bank_no, engine_copy) in enumerate(ways):
                cols = slice(n * width, (n + 1) * width)
                bank = psum.tile([P, width], F32, name=f"bank_{name}{t}{n}", tag=f"bank{bank_no}")
                multiply(bank[:], weight, slice(t * P, (t + 1) * P), x_mx, cols)
                engine_copy(rows[:, cols], bank[:])

        x_mx = operand("x", S)
        quantize(x_mx, flat(x_woven, 0, S), 0, S // 2)

        w1_woven = sbuf("w1_woven", [P, H * PACK], BF16)
        w2_woven = late.tile([P, H * PACK], BF16, name="w2_woven", offset=0, align_bytes=64)
        w1_mx = operand("w1", H)
        w2_mx = operand("w2", H)
        round_pair(nc.vector.tensor_copy, w1_woven, 0, w1_raw, 0, 0, W1_VECTOR_COLUMNS)
        round_pair(nc.scalar.copy, w1_woven, 0, w1_raw, 0, W1_VECTOR_COLUMNS, P)
        quantize(x_mx, flat(x_woven, 0, S), S // 2, 3 * S // 4)
        quantize(w1_mx, w1_woven[:], 0, P)
        quantize(x_mx, flat(x_woven, 0, S), 3 * S // 4, S)
        quantize(w1_mx, w1_woven[:], P, PAIR * P)
        round_pair(nc.scalar.copy, w1_woven, 0, w1_raw, 1, 0, P)
        round_pair(nc.scalar.copy, w2_woven, 0, w2_halves[0], 0, W2_VECTOR_COLUMNS, W2_CUT)
        round_pair(nc.vector.tensor_copy, w2_woven, 0, w2_halves[0], 0, 0, W2_VECTOR_COLUMNS)
        round_pair(nc.vector.tensor_copy, w2_woven, 0, w2_halves[0], 1, 0, W2_CUT)
        quantize(w1_mx, w1_woven[:], PAIR * P, H)
        for u in range(PACK // PAIR):
            round_pair(nc.vector.tensor_copy, w2_woven, W2_CUT, w2_halves[1], u, 0, P - W2_CUT)
        quantize(w2_mx, w2_woven[:], 0, P)
        quantize(w2_mx, w2_woven[:], P, H)

        centre = sbuf("centre", [P, PACK, V], F32)

        def centres(t, rows):
            scalar_gather(centre[:, t, :], rows.indirect(cen_sb[:]))

        y_rows = [sbuf(f"y_rows{t}", [P, S], F32) for t in range(PAIR)]
        y_rows.append(late.tile([P, S], F32, name="y_rows2", offset=0, align_bytes=64))
        later_edges = late.tile([P, PACK, 2 * V], F32, name="later_edges", offset=S * 4, align_bytes=64)
        y_rows = [rows[:] for rows in y_rows] + [later_edges[:, PAIR, :]]
        e_rows = [sbuf(f"e_rows{t}", [P, S], F32) for t in range(PACK)]
        on_scalar, on_vector = nc.scalar.copy, nc.vector.tensor_copy
        hidden_rows("y", w1_mx, 0, ((0, on_scalar), (1, on_scalar)), y_rows[0])
        hidden_rows("y", w1_mx, 1, ((2, on_scalar),), y_rows[1])
        centres(0, y_rows[0])
        centres(1, y_rows[1])
        hidden_rows("e", w2_mx, 0, ((5, on_vector), (6, on_vector)), e_rows[0])
        hidden_rows("e", w2_mx, 1, ((7, on_vector), (4, on_scalar)), e_rows[1])
        hidden_rows("y", w1_mx, 2, ((3, on_scalar),), y_rows[2])
        hidden_rows("e", w2_mx, 2, ((0, on_scalar),), e_rows[2])
        centres(2, y_rows[2])
        hidden_rows("y", w1_mx, 3, ((5, on_scalar),), y_rows[3])
        hidden_rows("e", w2_mx, 3, ((1, on_scalar),), e_rows[3])
        centres(3, y_rows[3])
        edge = (sbuf("edge0", [P, PACK, V], F32), later_edges[:, :, :V], later_edges[:, :, V:])
        for t in range(FETCHED):
            scalar_gather(edge[2][:, t, :], e_rows[t][:].indirect(pos_sb[2][:]))

        act = [sbuf(f"act{d}", [P, V, PACK], BF16) for d in range(3)]

        def edge_sums(d, lo, hi, tiles):
            for t in tiles:
                nc.vector.tensor_tensor(
                    edge[d][:, t, lo:hi], e_rows[t][:].indirect(entries(pos_sb[d], lo, hi)), centre[:, t, lo:hi], ADD
                )

        def gelu(d, lo, hi, run=RUN):
            nc.scalar.activation(
                act[d][:, lo:hi, :].rearrange("p (c i) t -> p c t i", i=run),
                edge[d][:, :, lo:hi].rearrange("p t (c i) -> p c t i", i=run),
                GELU,
            )

        halves = ((0, V // 2), (V // 2, V))
        for tiles in (range(PAIR), range(PAIR, PACK)):
            edge_sums(0, 0, V, tiles)
            edge_sums(1, 0, V, tiles)
        gelu(0, 0, V)
        gelu(1, 0, V)
        nc.vector.tensor_tensor(edge[2][:, :FETCHED, :], edge[2][:, :FETCHED, :], centre[:, :FETCHED, :], ADD)
        for lo, hi in halves:
            edge_sums(2, lo, hi, range(FETCHED, PACK))
            gelu(2, lo, hi, LINE_RUN)

        best_two = [sbuf(f"best_two{g}", [P, V // 2 * PACK], BF16) for g in range(2)]
        z = sbuf("z", [P, V, PACK], BF16)
        for g, (lo, hi) in enumerate(halves):
            nc.vector.tensor_tensor(best_two[g][:], flat(act[0], lo, hi), flat(act[1], lo, hi), MAX)
        for g, (lo, hi) in enumerate(halves):
            nc.vector.tensor_tensor(flat(z, lo, hi), best_two[g][:], flat(act[2], lo, hi), MAX)
        z_mx = [
            (late.tile([P, V // 2], U32, name="z0_codes", offset=S * 4, align_bytes=64), sbuf("z0_bytes", [P, V // 2], U8)),
            (sbuf("z1_codes", [P, V // 2], U32), sbuf("z1_bytes", [P, V // 2], U8)),
        ]
        for g, (lo, hi) in enumerate(halves):
            quantize(z_mx[g], flat(z, lo, hi), 0, hi - lo)

        ways_out = ((nc.vector.tensor_copy, nc.sync), (nc.scalar.copy, nc.scalar))
        out_banks = (2, 3, 4, 6)
        for g, (lo, hi) in enumerate(halves):
            for h, (engine_copy, queue) in enumerate(ways_out):
                bank = psum.tile([P, hi - lo], F32, name=f"out_bank{g}{h}", tag=f"bank{out_banks[2 * g + h]}")
                multiply(bank[:], (w3_codes, w3_bytes), slice(h * P, (h + 1) * P), z_mx[g], slice(0, hi - lo))
                staged = sbuf(f"staged{g}{h}", [P, hi - lo], F32)
                engine_copy(staged[:], bank[:])
                queue.dma_start(out[h * P : (h + 1) * P, lo:hi], staged[:])
